import numpy as np, ml_dtypes
CORES = [2,3,42,43,82,83,122,123]
N = 8
BF = ml_dtypes.bfloat16
def gentries(a):
    return np.ascontiguousarray(a.reshape(8, 16, -1).transpose(0, 2, 1)).reshape(8, -1)
def gtable(e):
    e = np.asarray(e); return np.ascontiguousarray(e.reshape(8, -1, 16).transpose(0, 2, 1)).reshape(128, -1).astype(np.int32)
I, V, G, M, RO = 1024, 353, 96, 1024, 3
def grow(J):
    T = J.shape[0]; ar = np.arange(T); ch = np.zeros((T, 2 * I), np.int64); free = np.zeros((T, I + 1), np.int64); free[:, 1] = 1
    for t in range(1, I):
        j = J[:, t]; ch[ar, free[ar, j]] = t; free[ar, j] = 2 * t; free[:, t + 1] = 2 * t + 1
    ch[ar[:, None], free] = I + np.arange(I + 1)[None, :]
    return ch.reshape(T, I, 2)
def trees(rng, kind, lab):
    T = N * 8; k = kind.reshape(T, 1); t = np.arange(I)[None, :]; r = rng.random((T, I))
    level = t + 1 - 2 ** (np.frexp((t + 1).astype(np.float64))[1].astype(np.int64) - 1)
    J = np.where(k == 0, (r * (t + 1)).astype(np.int64), np.where(k == 1, t - np.minimum((4 * r).astype(np.int64), t), np.where(k == 2, t, level)))
    ch = grow(J); b = lab.reshape(T, 1); s = np.arange(I + 1)[None, :]
    pi = np.where(b == 0, np.argsort(rng.random((T, I)), axis=1), np.where(b == 1, t, I - 1 - t))
    lf = I + np.where(b == 0, np.argsort(rng.random((T, I + 1)), axis=1), np.where(b == 1, s, I - s))
    c = np.take_along_axis(np.concatenate([pi, lf], axis=1), ch.reshape(T, 2 * I), 1).reshape(T, I, 2)
    c = np.where(rng.random((T, I, 1)) < 0.5, c[:, :, ::-1], c)
    o = np.zeros_like(c); o[np.arange(T)[:, None], pi] = c
    return o[:, :, 0].reshape(N, 8, I), o[:, :, 1].reshape(N, 8, I)
def parts(rng):
    size = rng.random((N, 8, 1, I + V)); size[..., :I] = 0.4 + 0.6 * size[..., :I]
    h = np.minimum((256 * size * rng.random((N, 8, 16, I + V))).astype(np.int64), 255)
    return h, rng.integers(-50, 51, (N, 8, 16, V)), rng.integers(0, V, (N, 8, N - 1, G))
def pack(h, v, tr, s):
    return {"h0": np.ascontiguousarray(h.reshape(N, 128, I + V)).astype(np.int32), "vel": np.ascontiguousarray(v.reshape(N, 128, V)).astype(np.int32),
            "kl": np.stack([gtable(a) for a in tr[0]]), "kr": np.stack([gtable(a) for a in tr[1]]), "sl": np.stack([gtable(a.reshape(8, -1)) for a in s])}
def setup_inputs(rng):
    h, v, s = parts(rng)
    return pack(h, v, trees(rng, rng.integers(0, 2, (N, 8)), np.zeros((N, 8), np.int64)), s)
def setup_inputs_ties(rng):
    h, v, s = parts(rng)
    h[:, ::2] = 8 * rng.integers(0, 4, (N, 4, 1, I + V)); h[:, ::2, :, :I] += 16
    v[:, ::2] = 8 * rng.integers(-1, 2, (N, 4, 1, V))
    h[:, 1::2] = 100 + (rng.random((N, 4, 16, I + V)) < 0.0625); v[:, 1::2] = rng.integers(-1, 2, (N, 4, 1, V))
    return pack(h, v, trees(rng, rng.integers(0, 4, (N, 8)), rng.integers(0, 3, (N, 8))), s)
def setup_inputs_chain(rng):
    h, v, s = parts(rng)
    kind = np.tile(np.array([2, 3, 2, 1, 2, 3, 2, 0]), (N, 1)); lab = rng.integers(0, 3, (N, 8)); lab[:, 0] = np.arange(N) % 3; lab[:, 4] = (np.arange(N) + 1) % 3
    for g in (0, 4): h[:, g, :, :I] = 255; h[:, g, :, I:] = 0
    lab[:, 2] = 1 + np.arange(N) % 2; node = np.arange(I)[None, :]
    depth = np.where(lab[:, 2:3] == 1, node, I - 1 - node)
    h[:, 2, :, :I] = rng.integers(0, 128, (N, 16, I)) + 128 * (depth % 2)[:, None, :]; h[:, 2, :, I:] = 0
    return pack(h, v, trees(rng, kind, lab), s)
def setup_inputs_edge(rng):
    h, v, s = parts(rng)
    h = 255 * (rng.random(h.shape) < rng.random((N, 8, 1, I + V))).astype(np.int64); h[:, 3, :, :I] = 255; h[:, 3, :, I:] = 0
    v = 127 * rng.integers(-1, 2, v.shape); s[:, ::2] = (V - 1) * rng.integers(0, 2, (N, 4, N - 1, G))
    lab = rng.integers(1, 3, (N, 8)); lab[:, 0] = 1; lab[:, 1] = 2
    tr = trees(rng, rng.integers(0, 4, (N, 8)), lab)
    c = np.stack([tr[0][0, 0], tr[1][0, 0]], axis=1)
    w = int(c[0][c[0] != 1][0]); low = np.concatenate([np.array([w]), c[1], c[w:w + 1].reshape(-1)]); low = low[low < I + V]
    h[0, 0][:, low] = 0; h[0, 0][:, 1] = 255
    return pack(h, v, tr, s)
def setup_inputs_alike(rng):
    h, v, s = parts(rng); kl, kr = trees(rng, np.zeros((N, 8), np.int64), np.zeros((N, 8), np.int64))
    kl[:] = kl[:, :1]; kr[:] = kr[:, :1]
    g = rng.permutation(8); h[:, g[0], :, :I] = 0; h[:, g[1:3]] = h[:, g[1:3], :1]
    s = rng.choice(np.array([0, V - 1, V // 2, 3]), s.shape)
    return pack(h, v, (kl, kr), s)
def setup_inputs_spread(rng):
    h, v, s = parts(rng)
    h = np.minimum((np.exp2(1 + 8 * rng.random((N, 8, 1, I + V))) * rng.random(h.shape)).astype(np.int64), 255)
    v = np.minimum((np.exp2(7 * rng.random((N, 8, 1, V))) * rng.random(v.shape)).astype(np.int64), 127) * (2 * rng.integers(0, 2, v.shape) - 1)
    return pack(h, v, trees(rng, rng.integers(0, 4, (N, 8)), np.zeros((N, 8), np.int64)), s)
def check_inputs(d):
    bad = []
    for k, lo, hi in (("h0", 0, 255), ("vel", -127, 127), ("kl", 0, 2 * I), ("kr", 0, 2 * I), ("sl", 0, V - 1)):
        if np.min(d[k]) < lo or np.max(d[k]) > hi: bad.append("range of " + k)
    if bad: return bad
    for q in range(N):
        c = np.concatenate([gentries(d["kl"][q]), gentries(d["kr"][q])], axis=1).astype(np.int64); o = np.sort(c, axis=1)
        if np.any(o[:, 1:] == o[:, :-1]):
            bad.append("children all differ"); break
        up = np.tile(np.arange(2 * I + 1), (8, 1)); np.put_along_axis(up, c, np.tile(np.arange(I), (8, 2)), 1)
        for i in range(13): up = np.take_along_axis(up, up, 1)
        if np.any(up != up[:, :1]):
            bad.append("one tree"); break
    return bad
def reference(h0, vel, kl, kr, sl):
    E = 2 * I + 1; at = np.arange(I)
    H = np.zeros((N, 8, 16, E), np.int64); H[..., :I + V] = h0.reshape(N, 8, 16, I + V)
    v = vel.astype(np.int64).reshape(N, 8, 16, V); s = np.stack([gentries(a) for a in sl]).astype(np.int64).reshape(N, 8, N - 1, G)
    K = np.stack([np.stack([gentries(kl[q]), gentries(kr[q])], axis=1) for q in range(N)]).astype(np.int64)
    for rnd in range(RO):
        for q in range(N):
            for d in range(1, N):
                o = (q - d) % N; j = I + V + (d - 1) * G
                H[q, :, :, j:j + G] = np.take_along_axis(H[o, :, :, I:I + V], s[o, :, d - 1][:, None, :], 2)
        hc = [np.take_along_axis(H, K[:, :, a][:, :, None, :], 3) for a in (0, 1)]
        best = np.zeros((N, 8, I), np.int64); ca = np.zeros_like(best); cb = np.zeros_like(best)
        for a in (0, 1):
            inner = K[:, :, a] < I; u = np.where(inner, K[:, :, a], 0); su = np.add.reduce(hc[a], axis=2)
            for b in (0, 1):
                z = np.take_along_axis(K[:, :, 1 - b], u, 2)
                gain = su - np.add.reduce(np.maximum(hc[1 - a], np.take_along_axis(H, z[:, :, None, :], 3)), axis=2)
                more = inner & (gain > best); best = np.where(more, gain, best); ca = np.where(more, a, ca); cb = np.where(more, b, cb)
        key = np.full((N, 8, E + 1), -1, np.int64); key[..., :I] = np.where(best > 0, M * best + at, -1)
        par = np.full((N, 8, E), E, np.int64)
        for a in (0, 1): np.put_along_axis(par, K[:, :, a], np.tile(at, (N, 8, 1)), 2)
        near = np.take_along_axis(key, par[..., :I], 2)
        for a in (0, 1): near = np.maximum(near, np.take_along_axis(key, K[:, :, a], 2))
        q, g, n = np.nonzero(key[..., :I] > near); a = ca[q, g, n]; b = cb[q, g, n]
        u = K[q, g, a, n]; w = K[q, g, 1 - a, n]; x = K[q, g, b, u]
        K[q, g, 1 - a, n] = x; K[q, g, b, u] = w
        new = np.maximum(np.take_along_axis(H, K[:, :, 0][:, :, None, :], 3), np.take_along_axis(H, K[:, :, 1][:, :, None, :], 3))
        H[..., I:I + V] = np.minimum(np.maximum(H[..., I:I + V] + v, 0), 255); H[..., :I] = new
    return {"yh": H[..., :I + V].reshape(N, 128, I + V).astype(np.float32), "yk": K.reshape(N, 8, 2 * I).astype(np.float32)}

@@ -1,0 +1,506 @@
+from concourse.bass import DstId, RemoteDMATransfer
+from concourse.mybir import AluOpType, ActivationFunctionType
+
+OP = AluOpType
+AF = ActivationFunctionType
+I, V0, GH, RO = 1024, 353, 96, 3
+LEAF = WIN = 2176
+
+SCRATCH = {"b%d" % _b: ("psum", [128, 512], "float32") for _b in range(8)}
+for _dt, _names in (
+        ("int32", "hl 360 hi 1024 vi 360 si 48 pi 8 pq 8 KI 128 gi 64"),
+        ("uint16", "su 48 KU 128 KB 128 PB 64 PPu 64"),
+        ("bfloat16", "HA 2064 HB 2064 vo 368 sh 672 sv 672 lh 672 lv 672 hcl 2176 hcr 2176 hr2 1024 mm 3072 zz 1024 rl 1024 rr 1024 "
+                     "GW 2176 CW 2176 gl 1024 gr 1024 gp 1024 cp 1024 cg 1024 ones 144 ec 144 ES 2304 bc 16 BS 144 BSn 144 sG 144 sL 144 "
+                     "sR 144 sS 144 sC 144 sC2 144 sPn 144 sPB 144 sRC 144 sO 144 id1 128 idn 128 idn16 128 id16 128 id64 128 id512 128 "
+                     "idnb 128 idh 128 idp 128 PW 2064 nrow 1024 chi 64 k129 64 sgn 128 CK 256 "
+                     "TB 192 CKP 128 ghi 64 glo 64 code 64 fh 128 fl 128 nch 128 cq 256"),
+        ("float32", "y1 1032 id32 128 qf 8 jr 16 oh 16 ww 16 c16 64 KF 128 PI 64 GPs 64 sib 64 sp 64 "
+                    "q1s 128 qm 128 qq 128 ga 64 cd 64 cc 64 tt 192 rot 64 MK 256 pr 256 xs 128 K1 128 dS 128 sd 128 ee 128 te 128 "
+                    "pt 512 OK 2048 OH 1384")):
+    _w = _names.split()
+    for _n, _c in zip(_w[::2], _w[1::2]):
+        SCRATCH[_n] = ("sbuf", [128, int(_c)], _dt)
+SEMAPHORES = ["V", "A", "P", "G", "arrH", "arrV", "sent"] + ["d%d" % _i for _i in range(16)]
+
+
+def sends(T, topo, q):
+    src = T.cores[q]
+    dst = {d: T.cores[(q + d) % 8] for d in range(1, 8)}
+    near = [d for d in dst if topo.chip(dst[d]) == topo.chip(src)]
+    far = [d for d in dst if d not in near]
+    pool = list(topo.engines(src, dst[far[0]]))
+
+    def direct(d):
+        a, b = topo.chip(src), topo.chip(dst[d])
+        return topo.mates(a, b) or topo.same_plane(a, b)
+    far.sort(key=lambda d: (direct(d), d))
+    out = {}
+    spare = len(pool) - len(far)
+    used = 0
+    for d in far:
+        k = 2 if spare > 0 else 1
+        spare -= k - 1
+        out[d] = pool[used:used + k]
+        used += k
+    rest = [e for e in topo.engines(src, dst[near[0]]) if e not in pool]
+    for j, d in enumerate(near):
+        out[d] = rest[j:j + 1]
+    return out
+
+
+def rank_program(g, core, T, topo):
+    rank = T.rank_of(core)
+    if rank is None:
+        return
+    queue = {"V": g.vector, "A": g.scalar, "P": g.tensor, "G": g, "S": g.sync}
+    cnt = {}
+    known = {q: {} for q in queue}
+    acc = {}
+    ndma = [0]
+
+    def psum(name):
+        return name[0] == "b" and name[1:].isdigit()
+
+    def hazards(q, rd, wr):
+        deps = []
+        for ops, w in ((rd, False), (wr, True)):
+            for _, name, a, b in ops:
+                if psum(name):
+                    deps += [r for qq, r in acc.setdefault(name, {}).items() if qq != q]
+                    continue
+                for k, x, y, r in acc.setdefault(name, []):
+                    if x < b and y > a and (w or k) and not (r[2] == q and (q == "P" or not k)):
+                        deps.append(r)
+        return deps
+
+    def note(q, rd, wr, rec):
+        for ops, w in ((rd, False), (wr, True)):
+            for _, name, a, b in ops:
+                if psum(name):
+                    acc[name][q] = rec
+                    continue
+                lst = acc[name]
+                if w:
+                    lst[:] = [t for t in lst if not (t[1] >= a and t[2] <= b)]
+                else:
+                    lst[:] = [t for t in lst if t[0] or t[3][2] != rec[2] or not (t[1] >= a and t[2] <= b)]
+                lst.append((w, a, b, rec))
+
+    def sync(q, deps):
+        kn = known[q]
+        best = {}
+        for r in deps:
+            if kn.get(r[0], 0) < r[1] and (r[0] not in best or best[r[0]][1] < r[1]):
+                best[r[0]] = r
+        for r in sorted(best.values(), key=lambda r: -len(r[3])):
+            if kn.get(r[0], 0) >= r[1]:
+                continue
+            queue[q].wait_ge(T.sem[r[0]], r[1])
+            for s, c in r[3].items():
+                kn[s] = max(kn.get(s, 0), c)
+            kn[r[0]] = r[1]
+
+    def emit(q, fns, rd, wr):
+        sync(q, hazards(q, rd, wr))
+        for f in fns:
+            f().then_inc(T.sem[q], 1)
+            cnt[q] = cnt.get(q, 0) + 1
+        note(q, rd, wr, (q, cnt[q], q, dict(known[q])))
+
+    def dma(q, out, in_, rd, wr):
+        sync(q, hazards(q, rd, wr))
+        s = "d%d" % ndma[0]
+        ndma[0] += 1
+        cnt[s] = 16
+        queue[q].dma_start(out, in_).then_inc(T.sem[s], 16)
+        note("D", rd, wr, (s, 16, "D", dict(known[q])))
+
+    def X(name, a, b, step=1):
+        return (T[name][:, a:b] if step == 1 else T[name][:, a:b:step], name, a, b)
+
+    def ind(win, off):
+        return (win[0].indirect(off[0]), win, off)
+
+    def flat(*ops):
+        out = []
+        for o in ops:
+            out += [o[1], o[2]] if len(o) == 3 else [o]
+        return out
+
+    def vcopy(out, in_):
+        if len(out) == 3:
+            emit("V", [lambda: g.vector.tensor_copy(out[0], in_[0])], [in_, out[2]], [out[1]])
+        else:
+            emit("V", [lambda: g.vector.tensor_copy(out[0], in_[0])], flat(in_), [out])
+
+    def vtt(out, a, b, op):
+        emit("V", [lambda: g.vector.tensor_tensor(out[0], a[0], b[0], op)], flat(a, b), [out])
+
+    def vts(out, a, s1, op0, s2=None, op1=None):
+        rd = [a] + [s for s in (s1, s2) if isinstance(s, tuple)]
+        v1 = s1[0] if isinstance(s1, tuple) else s1
+        v2 = s2[0] if isinstance(s2, tuple) else s2
+        if op1 is None:
+            emit("V", [lambda: g.vector.tensor_scalar(out[0], a[0], v1, None, op0)], rd, [out])
+        else:
+            emit("V", [lambda: g.vector.tensor_scalar(out[0], a[0], v1, v2, op0, op1)], rd, [out])
+
+    def vset(out, c):
+        emit("V", [lambda: g.vector.memset(out[0], c)], [], [out])
+
+    def act(out, in_, func=AF.Copy, scale=None, bias=None):
+        kw = {}
+        rd = flat(in_)
+        for key, v in (("scale", scale), ("bias", bias)):
+            if v is not None:
+                kw[key] = v[0] if isinstance(v, tuple) else v
+                rd = rd + ([v] if isinstance(v, tuple) else [])
+        emit("A", [lambda: g.scalar.activation(out[0], in_[0], func, **kw)], rd, [out])
+
+    def gsel(out, in_, pattern, op, base, cm):
+        emit("G", [lambda: g.affine_select(out[0], in_[0], pattern, op, 0.0, base, cm)], [in_], [out])
+
+    def giota(out, pattern, base, cm, flag):
+        kw = {"allow_small_or_imprecise_dtypes": True} if flag else {}
+        emit("G", [lambda: g.iota(out[0], pattern, base, cm, **kw)], [], [out])
+
+    def mm(out, lhsT, rhs, start, stop):
+        return lambda: g.tensor.matmul(out, lhsT, rhs, start, stop)
+
+    def wrap(bank, oc, strip, row, off=0, first=True, last=True, plus=()):
+        fns = []
+        rd = [X(strip, 0, 144), X(row, off, off + 1024)]
+        for j, (idm, buf, a) in enumerate(plus):
+            fns.append(mm(T[bank][:, oc:oc + 64], T[idm][:, 0:128], T[buf][:, a:a + 64], first and j == 0, False))
+            rd += [X(idm, 0, 128), X(buf, a, a + 64)]
+        for k in range(16):
+            fns.append(mm(T[bank][:, oc:oc + 64], T[strip][:, 16 - k:144 - k], T[row][:, off + k:off + 1024:16],
+                          first and not plus and k == 0, last and k == 15))
+        emit("P", fns, rd, [X(bank, oc, oc + 64)])
+
+    def full(bank, oc, terms, n, last=True, first=True):
+        fns = []
+        rd = []
+        for j, (idm, buf, a) in enumerate(terms):
+            fns.append(mm(T[bank][:, oc:oc + n], T[idm][:, 0:128], T[buf][:, a:a + n], first and j == 0, last and j == len(terms) - 1))
+            rd += [X(idm, 0, 128), X(buf, a, a + n)]
+        emit("P", fns, rd, [X(bank, oc, oc + n)])
+
+    def spread1(banks, h, parts, first, last):
+        fns = []
+        rd = [X("ES", 0, 2304)]
+        for j, (part, buf, col) in enumerate(parts):
+            for k in range(8 * h, 8 * h + 8):
+                fns.append(mm(T[banks[h]][:, 64 * (k % 8):64 * (k % 8) + 64], T.ES[:, 144 * k + 16 - part:144 * k + 144 - part],
+                              T[buf][:, col:col + 64], first and j == 0 and k % 8 == 0,
+                              last and j == len(parts) - 1 and k % 8 == 7))
+            rd.append(X(buf, col, col + 64))
+        emit("P", fns, rd, [X(banks[h], 0, 512)])
+
+    dma("S", T.hl[:, 0:V0], T.h0[:, I:I + V0], [], [X("hl", 0, V0)])
+    dma("A", T.si[:, 0:42], T.sl[:, :], [], [X("si", 0, 42)])
+    dma("S", T.KI[:, 0:64], T.kl[:, :], [], [X("KI", 0, 64)])
+    dma("A", T.KI[:, 64:128], T.kr[:, :], [], [X("KI", 64, 128)])
+    dma("S", T.vi[:, 0:V0], T.vel[:, :], [], [X("vi", 0, V0)])
+    dma("S", T.hi[:, :], T.h0[:, 0:I], [], [X("hi", 0, 1024)])
+
+    vset(X("ones", 0, 144), 1.0)
+    giota(X("pi", 0, 1), [[0, 1]], 0, 1, False)
+    giota(X("jr", 0, 16), [[1, 16]], 0, 0, True)
+    gsel(X("ec", 0, 144), X("ones", 0, 144), [[-1, 16], [-16, 9]], OP.is_equal, 16, 1)
+    gsel(X("bc", 0, 9), X("ones", 0, 9), [[-16, 9]], OP.is_ge, 16, 1)
+    gsel(X("bc", 0, 9), X("bc", 0, 9), [[16, 9]], OP.is_ge, -1, -1)
+    gsel(X("id1", 0, 128), X("ones", 0, 128), [[-1, 128]], OP.is_equal, 0, 1)
+    giota(X("c16", 0, 64), [[16, 64]], 0, 0, True)
+    giota(X("chi", 0, 64), [[1, 64]], 129, 0, True)
+    vset(X("BS", 0, 144), 0.0)
+    vset(X("ES", 0, 2304), 0.0)
+    vts(X("pq", 0, 1), X("pi", 0, 1), 15, OP.bitwise_and)
+    vcopy(X("qf", 0, 1), X("pq", 0, 1))
+    vts(X("oh", 0, 16), X("jr", 0, 16), X("qf", 0, 1), OP.is_equal)
+    vcopy(X("BS", 0, 144, 16), X("bc", 0, 9))
+    vcopy(X("ES", 0, 2304, 16), X("ec", 0, 144))
+    vcopy(X("HA", I, I + V0), X("hl", 0, V0))
+    vcopy(X("su", 0, 42), X("si", 0, 42))
+    act(X("nch", 64, 128), X("c16", 0, 64), AF.Identity, 0.0, X("qf", 0, 1))
+    act(X("sh", 0, 672), ind(X("HA", I, I + V0), X("su", 0, 42)))
+    vcopy(X("KU", 0, 128), X("KI", 0, 128))
+    vcopy(X("vo", 0, V0), X("vi", 0, V0))
+    vts(X("ww", 11, 12), X("oh", 0, 1), 256.0, OP.mult)
+    vts(X("ww", 9, 10), X("oh", 1, 2), 16.0, OP.mult, X("ww", 11, 12), OP.add)
+
+    mine = sends(T, topo, rank)
+    nsent = [0]
+
+    def exchange(buf, land, sem):
+        sync("G", hazards("G", [X(buf, 0, 672)], []))
+        tr = []
+        for d in range(1, 8):
+            rid, pid, _ = topo.addr(T.cores[(rank + d) % 8])
+            tr.append(RemoteDMATransfer(src=T[buf][:, GH * (d - 1):GH * d], dst=T[land][:, GH * (d - 1):GH * d],
+                                        dst_ids=[DstId(rid=rid, pnc=pid)], dma_engine_mask=sum(1 << e for e in mine[d]),
+                                        remote_sem=T.sem[sem]))
+            nsent[0] += len(mine[d])
+        g.remote_dma_fused(tr, local_sem=T.sem.sent)
+    exchange("sh", "lh", "arrH")
+
+    act(X("PW", 0, 1024), X("ES", 0, 1024), AF.Identity, 0.0, X("ww", 9, 10))
+    for h in range(2):
+        fns = []
+        for part, buf, col in ((0, "chi", 0), (1, "nch", 64)):
+            for k in range(16):
+                c = col + 32 * h
+                fns.append(mm(T["b%d" % h][:, k:512:16], T.ES[:, 144 * k + 16 - part:144 * k + 144 - part], T[buf][:, c:c + 32],
+                              part == 0 and k == 0, part == 1 and k == 15))
+        emit("P", fns, [X("ES", 0, 2304), X("chi", 0, 64), X("nch", 64, 128)], [X("b%d" % h, 0, 512)])
+    act(X("nrow", 0, 512), X("b0", 0, 512))
+    act(X("nrow", 512, 1024), X("b1", 0, 512))
+    act(X("sv", 0, 672), ind(X("vo", 0, V0), X("su", 0, 42)))
+    exchange("sv", "lv", "arrV")
+    narr = sum(len(sends(T, topo, (rank - d) % 8)[d]) for d in range(1, 8))
+    for land, sem in (("lh", "arrH"), ("lv", "arrV")):
+        cnt[sem] = narr
+        acc.setdefault(land, []).append((True, 0, 672, (sem, narr, "R", {})))
+
+    def scatter(a):
+        vcopy(ind(X("PW", 0, 2049), X("KU", a, a + 64)), X("nrow", 0, 1024))
+
+    vts(X("ww", 10, 11), X("oh", 1, 2), 129.0, OP.mult)
+    for j, a, w, b in ((0, ("oh", 0), 1.0, ("oh", 1)), (1, ("oh", 2), 16.0, ("oh", 3)), (2, ("oh", 4), 16.0, ("oh", 5)),
+                       (3, ("ww", 1), 1.0, ("ww", 2)), (4, ("oh", 1), 16.0, ("oh", 2)), (5, ("oh", 2), 64.0, ("oh", 1)),
+                       (6, ("oh", 3), 16.0, ("oh", 4)), (7, ("oh", 0), 1.0, ("oh", 0)), (8, ("oh", 2), 16.0, ("ww", 10))):
+        vts(X("ww", j, j + 1), X(a[0], a[1], a[1] + 1), w, OP.mult, X(b[0], b[1], b[1] + 1), OP.add)
+    vcopy(X("KF", 0, 128), X("KI", 0, 128))
+    vcopy(X("HA", 0, I), X("hi", 0, I))
+    for nm, w in (("idn", -1.0), ("idn16", -16.0), ("id64", 64.0), ("id32", 1.0), ("id512", 512.0), ("idnb", -4096.0),
+                  ("idh", 0.5), ("id16", 16.0)):
+        act(X(nm, 0, 128), X("id1", 0, 128), scale=w)
+    act(X("nch", 0, 64), X("c16", 0, 64))
+    gsel(X("idp", 0, 128), X("ones", 0, 128), [[-1, 16], [-16, 8]], OP.is_equal, 0, 1)
+    for nm in ("hcl", "hcr", "GW"):
+        giota(X(nm, 1024, LEAF), [[0, LEAF - 1024]], 0, 0, True)
+    act(X("BSn", 0, 144), X("BS", 0, 144), scale=-1.0)
+    for j, c in enumerate((0.0, 0.5, 0.25, 0.75)):
+        vset(X("cq", 64 * j, 64 * j + 64), c)
+    vset(X("k129", 0, 64), 129.0)
+    for nm, w in (("sG", ("ww", 0)), ("sL", ("ww", 1)), ("sR", ("ww", 2)), ("sS", ("ww", 3)), ("sC", ("oh", 0)), ("sO", ("oh", 1)),
+                  ("sC2", ("ww", 7)), ("sPn", ("ww", 4)), ("sPB", ("ww", 5)), ("sRC", ("ww", 6))):
+        act(X(nm, 0, 144), X("BS", 0, 144), scale=X(w[0], w[1], w[1] + 1))
+
+    P_ = X("PI", 0, 64)
+    OWN = [("idn", "nch", 0), ("idn", "nch", 64)]
+    TIE = ("idh", "ones", 0)
+
+    def pt(i):
+        return X("pt", 64 * i, 64 * i + 64)
+
+    def chunks():
+        vts(X("CK", 0, 128), X("KF", 0, 128), 0.0625, OP.mult, 128.53125, OP.add)
+        full("b4", 128, [("id32", "KF", 0), ("idn16", "CK", 0)], 128)
+        full("b4", 256, [("id32", "KF", 0)] + OWN, 64)
+        full("b4", 320, [("id32", "KF", 64)] + OWN, 64)
+        for h in range(2):
+            spread1(("b0", "b1"), h, [(2, "CK", 0), (4, "CK", 64)], True, False)
+
+    scatter(0)
+    chunks()
+    act(X("CK", 128, 256), X("b4", 128, 256), scale=1.0, bias=2064.0)
+    act(X("CW", 1024, LEAF), X("ES", 0, LEAF - 1024), AF.Identity, 0.0, X("ww", 8, 9))
+    scatter(64)
+    wrap("b6", 128, "sC", "PW")
+    wrap("b6", 192, "sO", "PW")
+    vcopy(X("CKP", 0, 128), X("b6", 128, 256))
+    full("b6", 0, [("id16", "CKP", 0), ("id1", "CKP", 64)], 64)
+    full("b6", 64, [("id1", "CKP", 0), ("id64", "CKP", 64)], 64)
+    full("b6", 384, [("id16", "CKP", 0), ("id1", "CKP", 64), ("idn16", "k129", 0)] + OWN, 64)
+    vts(X("PB", 0, 64), X("b6", 64, 128), -129.0, OP.add)
+    act(P_, X("b6", 0, 64), scale=1.0, bias=-2064.0)
+    act(X("TB", 128, 192), X("b6", 384, 448), AF.Sign)
+    vcopy(X("HA", I + V0, 2049), X("lh", 0, 672))
+
+    cur, nxt = "HA", "HB"
+    for r in range(RO):
+        last = r == RO - 1
+        win = X(cur, 0, 2049)
+        wl, wr = X("hcl", 0, 2049), X("hcr", 0, 2049)
+        act(X("hcl", 0, 1024), ind(win, X("KU", 0, 64)))
+        vcopy(X("hcr", 0, 1024), ind(win, X("KU", 64, 128)))
+        act(X("sgn", 0, 128), X("CK", 0, 128), AF.Sign, 1.0, -192.5)
+        act(X("TB", 0, 128), X("b4", 256, 384), AF.Sign)
+        for h in range(2):
+            spread1(("b0", "b1"), h, [(3, "CK", 128), (5, "CK", 192)], False, False)
+        if r:
+            wrap("b7", 128, "sC2", "cg", plus=[("idn", "ones", 0), ("idn", "ones", 0)])
+            wrap("b7", 192, "sRC", "cg", plus=[("idn16", "CKP", 0), ("idn", "CKP", 64)])
+        wrap("b4", 0, "BS", "hcl", 0, True, False)
+        full("b6", 0, [("idn", "cq", 128)], 128, False)
+        wrap("b6", 64, "BSn", "hcl", 0, False, False)
+        wrap("b4", 64, "BS", "hcr", 0, False, False)
+        full("b4", 0, [("idnb", "sgn", 0), ("idnb", "ones", 0)], 128, True, False)
+        full("b7", 0, [("id1", "CK", 0), ("id64", "CK", 128), ("id512", "sgn", 0)], 128)
+        act(X("zz", 0, 512), ind(wl, X("KU", 64, 96)))
+        act(X("zz", 512, 1024), ind(wl, X("KU", 96, 128)))
+        vtt(X("mm", 1024, 2048), ind(wr, X("KU", 64, 128)), X("hcl", 0, 1024), OP.max)
+        full("b2", 0, [("idn", "hcl", 0), ("id1", "zz", 0)], 512)
+        full("b3", 0, [("idn", "hcl", 512), ("id1", "zz", 512)], 512)
+        act(X("hr2", 0, 1024), X("hcr", 0, 1024))
+        act(X("rl", 0, 512), X("b2", 0, 512), AF.Relu)
+        act(X("rl", 512, 1024), X("b3", 0, 512), AF.Relu)
+        full("b5", 0, [("idn", "cq", 0)], 128, False)
+        vtt(X("mm", 2048, 3072), ind(wl, X("KU", 0, 64)), X("hcr", 0, 1024), OP.max)
+        wrap("b5", 64, "BSn", "mm", 1024, False, False)
+        wrap("b6", 64, "BSn", "rl", 0, False, False)
+        vtt(X("mm", 0, 1024), ind(wr, X("KU", 0, 64)), X("hr2", 0, 1024), OP.max)
+        wrap("b6", 0, "BSn", "mm", 2048, False, True)
+        act(X("q1s", 0, 128), X("b6", 0, 128))
+        wrap("b5", 0, "BSn", "mm", 0, False, True)
+        full("b2", 0, [("id1", cur, I), ("id1", "vo", 0)], V0)
+        act(X("y1", 0, V0), X("b2", 0, V0), AF.Relu, -1.0, 255.0)
+        if not last:
+            full("b3", 0, [("id1", cur, I + V0), ("id1", "lv", 0)], 336)
+            full("b6", 128, [("id1", cur, I + V0 + 336), ("id1", "lv", 336)], 336)
+            act(X("y1", V0, V0 + 336), X("b3", 0, 336), AF.Relu, -1.0, 255.0)
+            act(X("y1", V0 + 336, 1025), X("b6", 128, 464), AF.Relu, -1.0, 255.0)
+        vts(X("KB", 0, 128), X("b7", 0, 128), 383.0, OP.add)
+        if r:
+            vtt(pt(1), X("ee", 0, 64), X("ee", 64, 128), OP.add)
+            vtt(pt(3), X("b7", 128, 192), X("sd", 0, 64), OP.subtract)
+            vts(pt(4), X("b7", 192, 256), 0.0, OP.is_equal, 4.0, OP.mult)
+            vtt(pt(2), X("sib", 0, 64), P_, OP.subtract)
+            vtt(pt(1), pt(0), pt(1), OP.subtract)
+            vtt(pt(6), pt(3), pt(4), OP.is_equal)
+        vtt(X("qm", 0, 128), X("q1s", 0, 128), X("b5", 0, 128), OP.max)
+        vtt(X("qq", 0, 128), X("b4", 0, 128), X("qm", 0, 128), OP.add)
+        vtt(X("ghi", 0, 64), X("qq", 0, 64), X("qq", 64, 128), OP.max)
+        vtt(X("ga", 0, 64), X("qq", 0, 64), X("qq", 64, 128), OP.max)
+        vtt(X("glo", 0, 64), X("ga", 0, 64), X("ghi", 0, 64), OP.subtract)
+        for part, buf in ((0, "ghi"), (1, "glo")):
+            for h in range(2):
+                spread1(("b0", "b1"), h, [(part, buf, 0)], False, part == 1)
+        if not last:
+            spread1(("b2", "b3"), 0, [(3, "CK", 64), (4, "CK", 192)], True, False)
+        if r:
+            vtt(pt(2), pt(1), pt(2), OP.mult)
+            vtt(pt(6), pt(6), X("GPs", 0, 64), OP.mult)
+            vtt(pt(5), P_, pt(2), OP.add)
+            vtt(P_, pt(5), pt(6), OP.add)
+            vts(X("CKP", 0, 64), P_, 0.0625, OP.mult, 128.53125, OP.add)
+            full("b7", 320, [("id32", "PI", 0), ("idn16", "CKP", 0)], 64)
+            full("b7", 384, [("id32", "PI", 0)] + OWN, 64)
+        vts(X("gi", 0, 64), X("ga", 0, 64), 0.375, OP.add)
+        vtt(X("cd", 0, 64), X("gi", 0, 64), X("ga", 0, 64), OP.subtract)
+        if not last:
+            spread1(("b2", "b3"), 1, [(3, "CK", 64), (4, "CK", 192)], True, False)
+        if r:
+            vts(X("CKP", 64, 128), X("b7", 320, 384), 2064.0, OP.add)
+            full("b7", 320, [("id1", "CKP", 0), ("id64", "CKP", 64)], 64)
+        vts(X("cc", 0, 64), X("cd", 0, 64), 4.0, OP.mult, 1.0, OP.add)
+        act(X("GW", 0, 512), X("b0", 0, 512))
+        if not r:
+            vcopy(X("GW", 512, 1024), X("b1", 0, 512))
+        else:
+            act(X("GW", 512, 1024), X("b1", 0, 512))
+            vts(X("PB", 0, 64), X("b7", 320, 384), -129.0, OP.add)
+        gwin = X("GW", 0, WIN)
+
+        def gather(buf, lst, o, a, b, eng):
+            eng(X(buf, a, b), ind(gwin, X(lst, o + a // 16, o + b // 16)))
+
+        def xx(oc, strip, row, side):
+            wrap("b7", oc, strip, row, plus=[("idn16", "CK", 64 * side), ("idn", "CK", 128 + 64 * side)])
+
+        gather("gl", "KB", 0, 0, 512, act)
+        gather("gr", "KB", 64, 0, 512, act)
+        if not last:
+            for h in range(2):
+                spread1(("b2", "b3"), h, [(1, "CKP", 0), (2, "CKP", 64)], False, False)
+        gather("gl", "KB", 0, 512, 1024, vcopy)
+        gather("gr", "KB", 64, 512, 1024, vcopy)
+        wrap("b4", 0, "sG", "gl", plus=[("idh", "TB", 0), TIE])
+        wrap("b5", 0, "sG", "gr", plus=[("idh", "TB", 64), TIE])
+        gather("gp", "PB", 0, 512, 1024, vcopy)
+        if r:
+            act(X("TB", 128, 192), X("b7", 384, 448), AF.Sign)
+        gather("gp", "PB", 0, 0, 512, act)
+        vts(X("tt", 0, 64), X("b4", 0, 64), 1.0, OP.max)
+        vtt(X("tt", 64, 128), X("b5", 0, 64), X("tt", 0, 64), OP.max)
+        wrap("b6", 0, "sG", "gp", plus=[("idh", "TB", 128), TIE])
+        xx(64, "sL", "gl", 1)
+        xx(192, "sR", "gl", 1)
+        vtt(X("tt", 128, 192), X("b6", 0, 64), X("tt", 64, 128), OP.max)
+        vtt(X("rot", 0, 64), X("gi", 0, 64), X("tt", 128, 192), OP.is_ge)
+        vtt(X("code", 0, 64), X("rot", 0, 64), X("cc", 0, 64), OP.mult)
+        if last:
+            act(X("OH", I, I + V0), X("y1", 0, V0), AF.Relu, -1.0, 255.0)
+            dma("S", T.yh[:, I:I + V0], T.OH[:, I:I + V0], [X("OH", I, I + V0)], [])
+        else:
+            act(X(nxt, I, 2049), X("y1", 0, 1025), AF.Relu, -1.0, 255.0)
+        for h in range(2):
+            spread1(("b2", "b3"), h, [(0, "code", 0)], last, True)
+        xx(0, "sL", "gr", 0)
+        xx(128, "sR", "gr", 0)
+        wrap("b6", 320, "sR", "gp", plus=[("idn16", "k129", 0)] + OWN)
+        wrap("b6", 256, "sS", "gp", plus=[("idn16", "k129", 0), ("idn16", "k129", 0)] + OWN)
+        for j, c in enumerate((3, 1, 4, 2)):
+            vts(X("MK", 64 * j, 64 * j + 64), X("code", 0, 64), float(c), OP.is_equal)
+        act(X("CW", 0, 512), X("b2", 0, 512))
+        vcopy(X("CW", 512, 1024), X("b3", 0, 512))
+        cwin = X("CW", 0, WIN)
+        vcopy(X("cp", 768, 1024), ind(cwin, X("PB", 48, 64)))
+        act(X("cp", 0, 768), ind(cwin, X("PB", 0, 48)))
+        vtt(X("pr", 0, 256), X("b7", 0, 256), X("MK", 0, 256), OP.mult)
+        wrap("b5", 0, "sC", "cp", plus=[("idn", "ones", 0)])
+        if not last:
+            wrap("b4", 0, "sPB", "cp")
+            wrap("b4", 64, "sPn", "cp", plus=[("idn16", "CKP", 0), ("idn", "CKP", 64)])
+        vtt(X("xs", 0, 128), X("pr", 0, 128), X("pr", 128, 256), OP.add)
+        vtt(X("K1", 0, 128), X("KF", 0, 128), X("xs", 0, 128), OP.add)
+        vts(X("sd", 0, 64), X("b6", 320, 384), 0.0, OP.is_equal, 2.0, OP.mult)
+        vts(X("sd", 64, 128), X("sd", 0, 64), 1.0, OP.add)
+        vtt(X("dS", 0, 64), X("b6", 256, 320), X("KF", 0, 64), OP.subtract)
+        vtt(X("dS", 64, 128), X("b6", 256, 320), X("KF", 64, 128), OP.subtract)
+        vtt(X("ee", 0, 64), X("b5", 0, 64), X("sd", 0, 64), OP.is_equal)
+        vtt(X("ee", 64, 128), X("b5", 0, 64), X("sd", 64, 128), OP.is_equal)
+        vtt(X("te", 0, 128), X("ee", 0, 128), X("dS", 0, 128), OP.mult)
+        if not last:
+            vts(X("PPu", 0, 64), X("b4", 0, 64), -129.0, OP.add)
+            act(X("sib", 0, 64), X("b6", 256, 320))
+            act(X("GPs", 0, 64), X("b4", 64, 128))
+            act(X("sp", 0, 64), X("b5", 0, 64), AF.Sign, 1.0, 0.5)
+            act(pt(0), X("sp", 0, 64), AF.Relu)
+        vtt(X("KF", 0, 128), X("K1", 0, 128), X("te", 0, 128), OP.add)
+        vcopy(X("KU", 0, 128), X("KF", 0, 128))
+        if last:
+            act(X("fh", 0, 128), X("KF", 0, 128))
+            vtt(X("fl", 0, 128), X("KF", 0, 128), X("fh", 0, 128), OP.subtract)
+        act(X("rr", 0, 320), ind(win, X("KU", 64, 84)))
+        act(X("rr", 320, 640), ind(win, X("KU", 84, 104)))
+        vcopy(X("rr", 640, 1024), ind(win, X("KU", 104, 128)))
+        if not last:
+            chunks()
+            act(X("cg", 0, 512), ind(cwin, X("PPu", 0, 32)))
+            act(X("CK", 128, 256), X("b4", 128, 256), scale=1.0, bias=2064.0)
+            act(X("cg", 512, 1024), ind(cwin, X("PPu", 32, 64)))
+        dst = "OH" if last else nxt
+        for a, b in ((640, 1024), (0, 320), (320, 640)):
+            vtt(X(dst, a, b), ind(win, X("KU", a // 16, b // 16)), X("rr", a, b), OP.max)
+            if last:
+                dma("S", T.yh[:, a:b], T.OH[:, a:b], [X("OH", a, b)], [])
+        cur, nxt = nxt, cur
+
+    for b in range(4):
+        bank = "b%d" % b
+        o = X("OK", 512 * b, 512 * b + 512)
+        fns = []
+        for j, buf in enumerate(("fh", "fl")):
+            for k in range(16):
+                fns.append(mm(T[bank][0:8, k:512:16], T.idp[:, 8 * k:8 * k + 8], T[buf][:, 32 * b:32 * b + 32],
+                              j == 0 and k == 0, j == 1 and k == 15))
+        emit("P", fns, [X("idp", 0, 128), X("fh", 0, 128), X("fl", 0, 128)], [X(bank, 0, 512)])
+        emit("A", [lambda: g.scalar.activation(T.OK[0:8, 512 * b:512 * b + 512], T[bank][0:8, 0:512], AF.Copy)],
+             [X(bank, 0, 512)], [o])
+        dma("S", T.yk[:, 512 * b:512 * b + 512], T.OK[0:8, 512 * b:512 * b + 512], [o], [])
+    cnt["sent"] = nsent[0]
+    for s, c in cnt.items():
+        g.wait_ge(T.sem[s], c)

@@ -4,24 +4,29 @@ from concourse.mybir import AluOpType, ActivationFunctionType
 OP = AluOpType
 AF = ActivationFunctionType
 I, V0, GH, RO = 1024, 353, 96, 3
-LEAF = WIN = 2176
+D = 7
+OWN, GHO, WIN = I + D, I + V0 + D, 2049 + D
+KL, KR, P2, P3, P0, P1, TL, TR, PAR, W0, W1, XX = range(12)
+QA = 64
 
 SCRATCH = {"b%d" % _b: ("psum", [128, 512], "float32") for _b in range(8)}
 for _dt, _names in (
-        ("int32", "hl 360 hi 1024 vi 360 si 48 pi 8 pq 8 KI 128 gi 64"),
-        ("uint16", "su 48 KU 128 KB 128 PB 64 PPu 64"),
-        ("bfloat16", "HA 2064 HB 2064 vo 368 sh 672 sv 672 lh 672 lv 672 hcl 2176 hcr 2176 hr2 1024 mm 3072 zz 1024 rl 1024 rr 1024 "
-                     "GW 2176 CW 2176 gl 1024 gr 1024 gp 1024 cp 1024 cg 1024 ones 144 ec 144 ES 2304 bc 16 BS 144 BSn 144 sG 144 sL 144 "
-                     "sR 144 sS 144 sC 144 sC2 144 sPn 144 sPB 144 sRC 144 sO 144 id1 128 idn 128 idn16 128 id16 128 id64 128 id512 128 "
-                     "idnb 128 idh 128 idp 128 PW 2064 nrow 1024 chi 64 k129 64 sgn 128 CK 256 "
-                     "TB 192 CKP 128 ghi 64 glo 64 code 64 fh 128 fl 128 nch 128 cq 256"),
-        ("float32", "y1 1032 id32 128 qf 8 jr 16 oh 16 ww 16 c16 64 KF 128 PI 64 GPs 64 sib 64 sp 64 "
-                    "q1s 128 qm 128 qq 128 ga 64 cd 64 cc 64 tt 192 rot 64 MK 256 pr 256 xs 128 K1 128 dS 128 sd 128 ee 128 te 128 "
-                    "pt 512 OK 2048 OH 1384")):
+        ("int32", "hl 360 hi 1024 vi 360 si 48 KI 128 gi 64"),
+        ("uint16", "su 48 KU 128 PB 64 PPu 64"),
+        ("float16", "KW 272 nid 320"),
+        ("bfloat16", "H0 2064 H1 2064 H2 2064 vo 368 s0 672 s1 672 s2 672 hcl 2064 hcr 2064 hr2 1024 mm 4096 zz 2048 rr 1024 "
+                     "GW 2064 CW 2064 PW 2064 nrow 1024 gl 1024 gr 1024 gp 1024 cp 1024 cg 1024 ones 128 idn 128 idh 128 idhn 128 "
+                     "idq 128 ide 128 idf 128 idk 128 WP 32 WG 56 OC 24 WC 40 BS 16 sPP 144 CQ 256 CE 320 msk 256 TB 192 "
+                     "cod 64 MK 256 E1 128 E2 192"),
+        ("float32", "nf 64 gq 256 ee 192 y1 360 OK 1024 OH 1384")):
     _w = _names.split()
     for _n, _c in zip(_w[::2], _w[1::2]):
         SCRATCH[_n] = ("sbuf", [128, int(_c)], _dt)
-SEMAPHORES = ["V", "A", "P", "G", "arrH", "arrV", "sent"] + ["d%d" % _i for _i in range(16)]
+SCRATCH["L"] = ("sbuf", [128, 193, 8], "float16")
+SCRATCH["id1"] = ("sbuf", [128, 16, 8], "bfloat16")
+SCRATCH["XG"] = ("sbuf", [128, 8, 16, 8], "bfloat16")
+SCRATCH["XC"] = ("sbuf", [128, 8, 16, 8], "bfloat16")
+SEMAPHORES = ["V", "A", "P", "G", "arr0", "arr1", "arr2", "sent"] + ["d%d" % _i for _i in range(20)]
 
 
 def sends(T, topo, q):
@@ -119,6 +124,12 @@ def rank_program(g, core, T, topo):
     def X(name, a, b, step=1):
         return (T[name][:, a:b] if step == 1 else T[name][:, a:b:step], name, a, b)
 
+    def part(name, p):
+        return (T[name][:, :, p, :], name, p, p + 1)
+
+    def lists(a, n=1):
+        return (T.L[:, 16 * a + 1:16 * (a + n):2, :], "L", 128 * a + 8, 128 * (a + n))
+
     def ind(win, off):
         return (win[0].indirect(off[0]), win, off)
 
@@ -137,66 +148,50 @@ def rank_program(g, core, T, topo):
     def vtt(out, a, b, op):
         emit("V", [lambda: g.vector.tensor_tensor(out[0], a[0], b[0], op)], flat(a, b), [out])
 
-    def vts(out, a, s1, op0, s2=None, op1=None):
-        rd = [a] + [s for s in (s1, s2) if isinstance(s, tuple)]
-        v1 = s1[0] if isinstance(s1, tuple) else s1
-        v2 = s2[0] if isinstance(s2, tuple) else s2
-        if op1 is None:
-            emit("V", [lambda: g.vector.tensor_scalar(out[0], a[0], v1, None, op0)], rd, [out])
-        else:
-            emit("V", [lambda: g.vector.tensor_scalar(out[0], a[0], v1, v2, op0, op1)], rd, [out])
+    def vts(out, a, s1, op0):
+        emit("V", [lambda: g.vector.tensor_scalar(out[0], a[0], s1, None, op0)], [a], [out])
 
     def vset(out, c):
         emit("V", [lambda: g.vector.memset(out[0], c)], [], [out])
 
-    def act(out, in_, func=AF.Copy, scale=None, bias=None):
-        kw = {}
-        rd = flat(in_)
-        for key, v in (("scale", scale), ("bias", bias)):
-            if v is not None:
-                kw[key] = v[0] if isinstance(v, tuple) else v
-                rd = rd + ([v] if isinstance(v, tuple) else [])
-        emit("A", [lambda: g.scalar.activation(out[0], in_[0], func, **kw)], rd, [out])
+    def act(out, in_, func=AF.Copy, **kw):
+        emit("A", [lambda: g.scalar.activation(out[0], in_[0], func, **kw)], flat(in_), [out])
 
     def gsel(out, in_, pattern, op, base, cm):
         emit("G", [lambda: g.affine_select(out[0], in_[0], pattern, op, 0.0, base, cm)], [in_], [out])
 
-    def giota(out, pattern, base, cm, flag):
-        kw = {"allow_small_or_imprecise_dtypes": True} if flag else {}
-        emit("G", [lambda: g.iota(out[0], pattern, base, cm, **kw)], [], [out])
+    def giota(out, pattern, base, cm):
+        emit("G", [lambda: g.iota(out[0], pattern, base, cm, allow_small_or_imprecise_dtypes=True)], [], [out])
 
-    def mm(out, lhsT, rhs, start, stop):
-        return lambda: g.tensor.matmul(out, lhsT, rhs, start, stop)
+    ID = (T.id1[:, :, :], "id1", 0, 128)
+    opened = set()
 
-    def wrap(bank, oc, strip, row, off=0, first=True, last=True, plus=()):
+    def pe(bank, terms, rd, last):
         fns = []
-        rd = [X(strip, 0, 144), X(row, off, off + 1024)]
-        for j, (idm, buf, a) in enumerate(plus):
-            fns.append(mm(T[bank][:, oc:oc + 64], T[idm][:, 0:128], T[buf][:, a:a + 64], first and j == 0, False))
-            rd += [X(idm, 0, 128), X(buf, a, a + 64)]
-        for k in range(16):
-            fns.append(mm(T[bank][:, oc:oc + 64], T[strip][:, 16 - k:144 - k], T[row][:, off + k:off + 1024:16],
-                          first and not plus and k == 0, last and k == 15))
-        emit("P", fns, rd, [X(bank, oc, oc + 64)])
+        for j, (o, l, r) in enumerate(terms):
+            first = bank not in opened
+            opened.add(bank)
+            fns.append(lambda o=o, l=l, r=r, a=first, z=last and j == len(terms) - 1: g.tensor.matmul(o, l, r, a, z))
+        if last:
+            opened.discard(bank)
+        emit("P", fns, rd, [X(bank, 0, 512)])
 
-    def full(bank, oc, terms, n, last=True, first=True):
-        fns = []
-        rd = []
-        for j, (idm, buf, a) in enumerate(terms):
-            fns.append(mm(T[bank][:, oc:oc + n], T[idm][:, 0:128], T[buf][:, a:a + n], first and j == 0, last and j == len(terms) - 1))
-            rd += [X(idm, 0, 128), X(buf, a, a + n)]
-        emit("P", fns, rd, [X(bank, oc, oc + n)])
+    def plus(bank, terms, last=False):
+        dg = [ID if t[2] == "id1" else X(t[2], 0, 128) for t in terms]
+        pe(bank, [(T[bank][:, t[0]:t[0] + t[1]], d[0], t[3][0]) for t, d in zip(terms, dg)], dg + [t[3] for t in terms], last)
 
-    def spread1(banks, h, parts, first, last):
-        fns = []
-        rd = [X("ES", 0, 2304)]
-        for j, (part, buf, col) in enumerate(parts):
-            for k in range(8 * h, 8 * h + 8):
-                fns.append(mm(T[banks[h]][:, 64 * (k % 8):64 * (k % 8) + 64], T.ES[:, 144 * k + 16 - part:144 * k + 144 - part],
-                              T[buf][:, col:col + 64], first and j == 0 and k % 8 == 0,
-                              last and j == len(parts) - 1 and k % 8 == 7))
-            rd.append(X(buf, col, col + 64))
-        emit("P", fns, rd, [X(banks[h], 0, 512)])
+    def wrap(bank, oc, row, off, w, last=False, step=8, at=1, nq=128):
+        n = w[3] - w[2]
+        pe(bank, [(T[bank][0:nq, oc + at * b:oc + at * b + step * (n - 1) + 1:step], T[row][:, off + b:off + 8 * nq:8], w[0])
+                  for b in range(8)], [X(row, off, off + 8 * nq), w], last)
+
+    def spread(buf, h):
+        pe("b%d" % h, [(T["b%d" % h][:, b:512:8], T[buf][:, :, :, b], T.id1[:, 8 * h:8 * h + 8, :]) for b in range(8)],
+           [(None, buf, 0, 16), ID], True)
+
+    def aslist(bank, oc, which, last=False):
+        pe(bank, [(T[bank][:, oc:oc + 64], T.L[:, 16 * a + 1 - h:16 * a + 17 - h, :], T.id1[:, :, h::2]) for a in which for h in range(2)],
+           [lists(a) for a in which] + [ID], last)
 
     dma("S", T.hl[:, 0:V0], T.h0[:, I:I + V0], [], [X("hl", 0, V0)])
     dma("A", T.si[:, 0:42], T.sl[:, :], [], [X("si", 0, 42)])
@@ -205,302 +200,283 @@ def rank_program(g, core, T, topo):
     dma("S", T.vi[:, 0:V0], T.vel[:, :], [], [X("vi", 0, V0)])
     dma("S", T.hi[:, :], T.h0[:, 0:I], [], [X("hi", 0, 1024)])
 
-    vset(X("ones", 0, 144), 1.0)
-    giota(X("pi", 0, 1), [[0, 1]], 0, 1, False)
-    giota(X("jr", 0, 16), [[1, 16]], 0, 0, True)
-    gsel(X("ec", 0, 144), X("ones", 0, 144), [[-1, 16], [-16, 9]], OP.is_equal, 16, 1)
-    gsel(X("bc", 0, 9), X("ones", 0, 9), [[-16, 9]], OP.is_ge, 16, 1)
-    gsel(X("bc", 0, 9), X("bc", 0, 9), [[16, 9]], OP.is_ge, -1, -1)
-    gsel(X("id1", 0, 128), X("ones", 0, 128), [[-1, 128]], OP.is_equal, 0, 1)
-    giota(X("c16", 0, 64), [[16, 64]], 0, 0, True)
-    giota(X("chi", 0, 64), [[1, 64]], 129, 0, True)
-    vset(X("BS", 0, 144), 0.0)
-    vset(X("ES", 0, 2304), 0.0)
-    vts(X("pq", 0, 1), X("pi", 0, 1), 15, OP.bitwise_and)
-    vcopy(X("qf", 0, 1), X("pq", 0, 1))
-    vts(X("oh", 0, 16), X("jr", 0, 16), X("qf", 0, 1), OP.is_equal)
-    vcopy(X("BS", 0, 144, 16), X("bc", 0, 9))
-    vcopy(X("ES", 0, 2304, 16), X("ec", 0, 144))
-    vcopy(X("HA", I, I + V0), X("hl", 0, V0))
-    vcopy(X("su", 0, 42), X("si", 0, 42))
-    act(X("nch", 64, 128), X("c16", 0, 64), AF.Identity, 0.0, X("qf", 0, 1))
-    act(X("sh", 0, 672), ind(X("HA", I, I + V0), X("su", 0, 42)))
-    vcopy(X("KU", 0, 128), X("KI", 0, 128))
-    vcopy(X("vo", 0, V0), X("vi", 0, V0))
-    vts(X("ww", 11, 12), X("oh", 0, 1), 256.0, OP.mult)
-    vts(X("ww", 9, 10), X("oh", 1, 2), 16.0, OP.mult, X("ww", 11, 12), OP.add)
+    vset(X("ones", 0, 128), 1.0)
+    giota(X("nf", 0, 64), [[0, 8], [1, 8]], -2048, 8)
+    gsel(ID, X("ones", 0, 128), [[-1, 128]], OP.is_equal, 0, 1)
+    emit("V", [lambda: g.vector.memset(T.XC[:], 0.0)], [], [(None, "XC", 0, 16)])
+    vcopy(part("XC", 0), X("nf", 0, 64))
+    vtt(part("XC", 1), X("nf", 0, 64), part("XC", 0), OP.subtract)
+    for h in range(2):
+        spread("XC", h)
+    vset(X("PW", 0, 1040), 0.0)
+    for r in range(RO):
+        vset(X("H%d" % r, I, OWN), 0.0)
+    vset(X("KW", 0, 272), 0.0)
+    emit("V", [lambda: g.vector.memset(T.L[:, 0:193:2, :], 0.0)], [], [(None, "L", 0, 1544)])
+    gsel(X("WP", 0, 32), X("ones", 0, 32), [[-2, 4], [-16, 8]], OP.is_ge, 0, 1)
+    gsel(X("WP", 0, 32), X("WP", 0, 32), [[2, 4], [16, 8]], OP.is_ge, 1, -1)
+    gsel(X("BS", 0, 8), X("ones", 0, 8), [[-16, 8]], OP.is_ge, 0, 1)
+    gsel(X("BS", 0, 8), X("BS", 0, 8), [[16, 8]], OP.is_ge, 15, -1)
+    for nm in ("H0", "H1", "H2", "hcl", "hcr", "GW", "CW"):
+        giota(X(nm, 0, D), [[0, D]], 0, 0)
+    emit("V", [lambda: g.vector.memset(T.XG[:], 0.0)], [], [(None, "XG", 0, 16)])
+    act(X("nrow", 0, 512), X("b0", 0, 512))
+    act(X("nrow", 512, 1024), X("b1", 0, 512))
+    vts(X("su", 0, 42), X("si", 0, 42), float(D), OP.add)
+    vcopy(X("H0", OWN, GHO), X("hl", 0, V0))
+    act(X("s0", 0, 320), ind(X("H0", I, GHO), X("su", 0, 20)))
+    vcopy(X("s0", 320, 672), ind(X("H0", I, GHO), X("su", 20, 42)))
+    vts(X("KU", 0, 128), X("KI", 0, 128), float(D), OP.add)
 
     mine = sends(T, topo, rank)
+    narr = sum(len(sends(T, topo, (rank - d) % 8)[d]) for d in range(1, 8))
     nsent = [0]
+    for r in range(RO):
+        cnt["arr%d" % r] = narr
+        acc.setdefault("H%d" % r, []).append((True, GHO, WIN, ("arr%d" % r, narr, "R", {})))
 
-    def exchange(buf, land, sem):
-        sync("G", hazards("G", [X(buf, 0, 672)], []))
+    def exchange(r):
+        sync("G", hazards("G", [X("s%d" % r, 0, 672)], []))
         tr = []
         for d in range(1, 8):
             rid, pid, _ = topo.addr(T.cores[(rank + d) % 8])
-            tr.append(RemoteDMATransfer(src=T[buf][:, GH * (d - 1):GH * d], dst=T[land][:, GH * (d - 1):GH * d],
+            tr.append(RemoteDMATransfer(src=T["s%d" % r][:, GH * (d - 1):GH * d], dst=T["H%d" % r][:, GHO + GH * (d - 1):GHO + GH * d],
                                         dst_ids=[DstId(rid=rid, pnc=pid)], dma_engine_mask=sum(1 << e for e in mine[d]),
-                                        remote_sem=T.sem[sem]))
+                                        remote_sem=T.sem["arr%d" % r]))
             nsent[0] += len(mine[d])
         g.remote_dma_fused(tr, local_sem=T.sem.sent)
-    exchange("sh", "lh", "arrH")
-
-    act(X("PW", 0, 1024), X("ES", 0, 1024), AF.Identity, 0.0, X("ww", 9, 10))
-    for h in range(2):
-        fns = []
-        for part, buf, col in ((0, "chi", 0), (1, "nch", 64)):
-            for k in range(16):
-                c = col + 32 * h
-                fns.append(mm(T["b%d" % h][:, k:512:16], T.ES[:, 144 * k + 16 - part:144 * k + 144 - part], T[buf][:, c:c + 32],
-                              part == 0 and k == 0, part == 1 and k == 15))
-        emit("P", fns, [X("ES", 0, 2304), X("chi", 0, 64), X("nch", 64, 128)], [X("b%d" % h, 0, 512)])
-    act(X("nrow", 0, 512), X("b0", 0, 512))
-    act(X("nrow", 512, 1024), X("b1", 0, 512))
-    act(X("sv", 0, 672), ind(X("vo", 0, V0), X("su", 0, 42)))
-    exchange("sv", "lv", "arrV")
-    narr = sum(len(sends(T, topo, (rank - d) % 8)[d]) for d in range(1, 8))
-    for land, sem in (("lh", "arrH"), ("lv", "arrV")):
-        cnt[sem] = narr
-        acc.setdefault(land, []).append((True, 0, 672, (sem, narr, "R", {})))
+    exchange(0)
+    gsel(X("vo", 0, V0), X("vi", 0, V0), [[0, V0]], OP.is_ge, 0, 0)
+    gsel(X("H0", D, OWN), X("hi", 0, I), [[0, I]], OP.is_ge, 0, 0)
 
     def scatter(a):
-        vcopy(ind(X("PW", 0, 2049), X("KU", a, a + 64)), X("nrow", 0, 1024))
-
-    vts(X("ww", 10, 11), X("oh", 1, 2), 129.0, OP.mult)
-    for j, a, w, b in ((0, ("oh", 0), 1.0, ("oh", 1)), (1, ("oh", 2), 16.0, ("oh", 3)), (2, ("oh", 4), 16.0, ("oh", 5)),
-                       (3, ("ww", 1), 1.0, ("ww", 2)), (4, ("oh", 1), 16.0, ("oh", 2)), (5, ("oh", 2), 64.0, ("oh", 1)),
-                       (6, ("oh", 3), 16.0, ("oh", 4)), (7, ("oh", 0), 1.0, ("oh", 0)), (8, ("oh", 2), 16.0, ("ww", 10))):
-        vts(X("ww", j, j + 1), X(a[0], a[1], a[1] + 1), w, OP.mult, X(b[0], b[1], b[1] + 1), OP.add)
-    vcopy(X("KF", 0, 128), X("KI", 0, 128))
-    vcopy(X("HA", 0, I), X("hi", 0, I))
-    for nm, w in (("idn", -1.0), ("idn16", -16.0), ("id64", 64.0), ("id32", 1.0), ("id512", 512.0), ("idnb", -4096.0),
-                  ("idh", 0.5), ("id16", 16.0)):
-        act(X(nm, 0, 128), X("id1", 0, 128), scale=w)
-    act(X("nch", 0, 64), X("c16", 0, 64))
-    gsel(X("idp", 0, 128), X("ones", 0, 128), [[-1, 16], [-16, 8]], OP.is_equal, 0, 1)
-    for nm in ("hcl", "hcr", "GW"):
-        giota(X(nm, 1024, LEAF), [[0, LEAF - 1024]], 0, 0, True)
-    act(X("BSn", 0, 144), X("BS", 0, 144), scale=-1.0)
-    for j, c in enumerate((0.0, 0.5, 0.25, 0.75)):
-        vset(X("cq", 64 * j, 64 * j + 64), c)
-    vset(X("k129", 0, 64), 129.0)
-    for nm, w in (("sG", ("ww", 0)), ("sL", ("ww", 1)), ("sR", ("ww", 2)), ("sS", ("ww", 3)), ("sC", ("oh", 0)), ("sO", ("oh", 1)),
-                  ("sC2", ("ww", 7)), ("sPn", ("ww", 4)), ("sPB", ("ww", 5)), ("sRC", ("ww", 6))):
-        act(X(nm, 0, 144), X("BS", 0, 144), scale=X(w[0], w[1], w[1] + 1))
-
-    P_ = X("PI", 0, 64)
-    OWN = [("idn", "nch", 0), ("idn", "nch", 64)]
-    TIE = ("idh", "ones", 0)
-
-    def pt(i):
-        return X("pt", 64 * i, 64 * i + 64)
-
-    def chunks():
-        vts(X("CK", 0, 128), X("KF", 0, 128), 0.0625, OP.mult, 128.53125, OP.add)
-        full("b4", 128, [("id32", "KF", 0), ("idn16", "CK", 0)], 128)
-        full("b4", 256, [("id32", "KF", 0)] + OWN, 64)
-        full("b4", 320, [("id32", "KF", 64)] + OWN, 64)
-        for h in range(2):
-            spread1(("b0", "b1"), h, [(2, "CK", 0), (4, "CK", 64)], True, False)
+        vcopy(ind(X("PW", 0, WIN), X("KU", a, a + 64)), X("nrow", 0, 1024))
 
     scatter(0)
-    chunks()
-    act(X("CK", 128, 256), X("b4", 128, 256), scale=1.0, bias=2064.0)
-    act(X("CW", 1024, LEAF), X("ES", 0, LEAF - 1024), AF.Identity, 0.0, X("ww", 8, 9))
+    for s in range(2):
+        vcopy(X("KW", 136 * s + 1, 136 * s + 129, 2), X("KI", 64 * s, 64 * s + 64))
+    vts(X("nid", 0, 64), X("nf", 0, 64), 2048.0, OP.add)
     scatter(64)
-    wrap("b6", 128, "sC", "PW")
-    wrap("b6", 192, "sO", "PW")
-    vcopy(X("CKP", 0, 128), X("b6", 128, 256))
-    full("b6", 0, [("id16", "CKP", 0), ("id1", "CKP", 64)], 64)
-    full("b6", 64, [("id1", "CKP", 0), ("id64", "CKP", 64)], 64)
-    full("b6", 384, [("id16", "CKP", 0), ("id1", "CKP", 64), ("idn16", "k129", 0)] + OWN, 64)
-    vts(X("PB", 0, 64), X("b6", 64, 128), -129.0, OP.add)
-    act(P_, X("b6", 0, 64), scale=1.0, bias=-2064.0)
-    act(X("TB", 128, 192), X("b6", 384, 448), AF.Sign)
-    vcopy(X("HA", I + V0, 2049), X("lh", 0, 672))
+    for nm, w in (("idn", -1.0), ("idh", 0.5), ("idhn", -0.5), ("idq", -0.25), ("ide", 2.0 ** -13), ("idf", -2.0 ** -14),
+                  ("idk", -2048.0)):
+        act(X(nm, 0, 128), ID, scale=w)
+    for nm in ("hcl", "hcr"):
+        act(X(nm, OWN, OWN + 1024), X("nrow", 0, 1024), scale=0.0, bias=255.0)
+        act(X(nm, WIN - 1, WIN), X("nrow", 0, 1), scale=0.0, bias=255.0)
 
-    cur, nxt = "HA", "HB"
+    def leaves(r):
+        plus("b2", [(0, V0, "id1", X("H%d" % r, OWN, GHO)), (0, V0, "id1", X("vo", 0, V0))], True)
+        act(X("y1", 0, V0), X("b2", 0, V0), AF.Relu, scale=-1.0, bias=255.0)
+        act(X("OH", I, I + V0) if r == RO - 1 else X("H%d" % (r + 1), OWN, GHO), X("y1", 0, V0), AF.Relu, scale=-1.0, bias=255.0)
+
+    for r in range(1, RO):
+        leaves(r - 1)
+        act(X("s%d" % r, 0, 672), ind(X("H%d" % r, I, GHO), X("su", 0, 42)))
+        if r == 1:
+            giota(X("CQ", 0, 256), [[0, 64], [1, 4]], 0, 0)
+        exchange(r)
+        giota(X("GW" if r == 1 else "CW", OWN, WIN), [[0, WIN - OWN]], 0, 0)
+    leaves(RO - 1)
+    dma("S", T.yh[:, I:I + V0], T.OH[:, I:I + V0], [X("OH", I, I + V0)], [])
+    giota(X("CE", 0, 256), [[1, 4], [0, 64]], -4, 0)
+    gsel(X("WG", 16, 48), X("ones", 0, 32), [[0, 4], [-16, 8]], OP.is_ge, -2, 1)
+    gsel(X("WG", 16, 48), X("WG", 16, 48), [[0, 4], [16, 8]], OP.is_ge, 5, -1)
+    giota(X("WC", 0, 32), [[0, 4], [-32, 8]], -1, 2)
+    gsel(X("WC", 0, 32), X("WC", 0, 32), [[0, 4], [-16, 8]], OP.is_ge, 0, 1)
+    gsel(X("WC", 0, 32), X("WC", 0, 32), [[0, 4], [16, 8]], OP.is_ge, 1, -1)
+    gsel(X("OC", 0, 8), X("ones", 0, 8), [[-16, 8]], OP.is_equal, -2, 1)
+
+    NID = X("nid", 0, 64)
+    ONE = X("ones", 0, 64)
+
+    def children(oc, first, last):
+        if first:
+            pe("b5", [(T.b5[:, oc + 64 * s:oc + 64 * s + 64], T.KW[:, 136 * s + 1 - h:136 * s + 129 - h], T.id1[:, h::2, :])
+                      for s in range(2) for h in range(2)], [X("KW", 0, 272), ID], last)
+        else:
+            plus("b5", [(oc, 128, "id1", lists(KL, 2)), (oc, 64, "id1", lists(P2)), (oc, 64, "id1", lists(P3)),
+                        (oc + 64, 64, "id1", lists(P0)), (oc + 64, 64, "id1", lists(P1)), (oc, 128, "id1", lists(TL, 2))], last)
+
+    def child_parts(first):
+        children(128, first, False)
+        plus("b5", [(128, 64, "idn", NID), (192, 64, "idn", NID)], True)
+        act(part("XG", 2), X("b5", 0, 64))
+        act(part("XG", 4), X("b5", 64, 128))
+        act(X("TB", 0, 128), X("b5", 128, 256), AF.Sign)
+        children(256, first, False)
+        plus("b5", [(256, 64, "idn", part("XG", 2)), (320, 64, "idn", part("XG", 4))], True)
+        act(part("XG", 3), X("b5", 256, 320))
+        act(part("XG", 5), X("b5", 320, 384))
+
+    def parents(oc, first):
+        if first:
+            wrap("b6", oc, "PW", D, X("WP", 0, 8))
+        else:
+            plus("b6", [(oc, 64, "id1", lists(a)) for a in (PAR, W0, W1, XX)])
+
+    def parent_parts(first):
+        parents(64, first)
+        parents(128, first)
+        if not first:
+            aslist("b6", 0, (PAR, W0, W1, XX))
+        plus("b6", [(128, 64, "idn", NID)], True)
+        act(part("XG", 6), X("b6", 64, 128))
+        act(X("TB", 128, 192), X("b6", 128, 192), AF.Sign, bias=2048.0)
+        parents(192, first)
+        plus("b6", [(192, 64, "idn", part("XG", 6))], True)
+        act(part("XG", 7), X("b6", 192, 256))
+
+    children(0, True, False)
+    child_parts(True)
+    act(X("BS", 8, 16), X("BS", 0, 8), scale=-1.0)
+    act(X("msk", 0, 256), X("CQ", 0, 256), AF.Sign)
+    parent_parts(True)
+    act(X("WG", 0, 8), X("WP", 0, 8), scale=-2.0 ** -13)
+    act(X("WG", 8, 16), X("WP", 16, 24))
+    act(X("WG", 48, 56), X("WP", 24, 32))
+    vcopy(lists(KL, 2), X("b5", 0, 128))
+    vset(X("sPP", 0, 144), 0.0)
+    vcopy(X("sPP", 16, 144, 16), X("WP", 24, 32))
+
+    BSP, BSN = X("BS", 0, 8), X("BS", 8, 16)
+    GA = X("gq", 3, 256, 4)
+    NA = 8 * QA
     for r in range(RO):
         last = r == RO - 1
-        win = X(cur, 0, 2049)
-        wl, wr = X("hcl", 0, 2049), X("hcr", 0, 2049)
-        act(X("hcl", 0, 1024), ind(win, X("KU", 0, 64)))
-        vcopy(X("hcr", 0, 1024), ind(win, X("KU", 64, 128)))
-        act(X("sgn", 0, 128), X("CK", 0, 128), AF.Sign, 1.0, -192.5)
-        act(X("TB", 0, 128), X("b4", 256, 384), AF.Sign)
-        for h in range(2):
-            spread1(("b0", "b1"), h, [(3, "CK", 128), (5, "CK", 192)], False, False)
+        win = X("H%d" % r, 0, WIN)
+        wl, wr = X("hcl", 0, WIN), X("hcr", 0, WIN)
+
+        def gain(row, off, w, ch, end=False, nq=128):
+            wrap("b4", ch, row, off, w, end, 32, 4, nq)
+
+        act(X("hcl", D, OWN), ind(win, X("KU", 0, 64)))
+        vcopy(X("hcr", D, OWN), ind(win, X("KU", 64, 128)))
         if r:
-            wrap("b7", 128, "sC2", "cg", plus=[("idn", "ones", 0), ("idn", "ones", 0)])
-            wrap("b7", 192, "sRC", "cg", plus=[("idn16", "CKP", 0), ("idn", "CKP", 64)])
-        wrap("b4", 0, "BS", "hcl", 0, True, False)
-        full("b6", 0, [("idn", "cq", 128)], 128, False)
-        wrap("b6", 64, "BSn", "hcl", 0, False, False)
-        wrap("b4", 64, "BS", "hcr", 0, False, False)
-        full("b4", 0, [("idnb", "sgn", 0), ("idnb", "ones", 0)], 128, True, False)
-        full("b7", 0, [("id1", "CK", 0), ("id64", "CK", 128), ("id512", "sgn", 0)], 128)
+            vts(X("E2", 0, 192), X("b3", 0, 192), 0.0, OP.is_equal)
+            vtt(lists(W0, 3), X("b7", 256, 448), X("E2", 0, 192), OP.mult)
+        vcopy(X("hr2", NA, 1024), X("hcr", D + NA, OWN))
+        plus("b4", [(0, 256, "idq", X("CQ", 0, 256))])
         act(X("zz", 0, 512), ind(wl, X("KU", 64, 96)))
         act(X("zz", 512, 1024), ind(wl, X("KU", 96, 128)))
-        vtt(X("mm", 1024, 2048), ind(wr, X("KU", 64, 128)), X("hcl", 0, 1024), OP.max)
-        full("b2", 0, [("idn", "hcl", 0), ("id1", "zz", 0)], 512)
-        full("b3", 0, [("idn", "hcl", 512), ("id1", "zz", 512)], 512)
-        act(X("hr2", 0, 1024), X("hcr", 0, 1024))
-        act(X("rl", 0, 512), X("b2", 0, 512), AF.Relu)
-        act(X("rl", 512, 1024), X("b3", 0, 512), AF.Relu)
-        full("b5", 0, [("idn", "cq", 0)], 128, False)
-        vtt(X("mm", 2048, 3072), ind(wl, X("KU", 0, 64)), X("hcr", 0, 1024), OP.max)
-        wrap("b5", 64, "BSn", "mm", 1024, False, False)
-        wrap("b6", 64, "BSn", "rl", 0, False, False)
-        vtt(X("mm", 0, 1024), ind(wr, X("KU", 0, 64)), X("hr2", 0, 1024), OP.max)
-        wrap("b6", 0, "BSn", "mm", 2048, False, True)
-        act(X("q1s", 0, 128), X("b6", 0, 128))
-        wrap("b5", 0, "BSn", "mm", 0, False, True)
-        full("b2", 0, [("id1", cur, I), ("id1", "vo", 0)], V0)
-        act(X("y1", 0, V0), X("b2", 0, V0), AF.Relu, -1.0, 255.0)
-        if not last:
-            full("b3", 0, [("id1", cur, I + V0), ("id1", "lv", 0)], 336)
-            full("b6", 128, [("id1", cur, I + V0 + 336), ("id1", "lv", 336)], 336)
-            act(X("y1", V0, V0 + 336), X("b3", 0, 336), AF.Relu, -1.0, 255.0)
-            act(X("y1", V0 + 336, 1025), X("b6", 128, 464), AF.Relu, -1.0, 255.0)
-        vts(X("KB", 0, 128), X("b7", 0, 128), 383.0, OP.add)
+        act(X("zz", 1024, 1024 + NA), ind(wr, X("KU", 0, NA // 16)))
+        vtt(X("mm", 1024, 2048), ind(wl, X("KU", 0, 64)), X("hcr", D, OWN), OP.max)
+        vtt(X("mm", 2048, 3072), ind(wr, X("KU", 64, 128)), X("hcl", D, OWN), OP.max)
+        vtt(X("mm", NA, 1024), ind(wr, X("KU", NA // 16, 64)), X("hr2", NA, 1024), OP.max)
+        gain("hcl", D, BSP, 0)
+        gain("hcl", D, BSP, 1)
+        plus("b0", [(0, 512, "idn", X("hcl", D, D + 512)), (0, 512, "id1", X("zz", 0, 512))], True)
+        gain("hcl", D, BSN, 3)
+        gain("hcr", D, BSP, 2)
+        plus("b1", [(0, 512, "idn", X("hcl", D + 512, OWN)), (0, 512, "id1", X("zz", 512, 1024))], True)
+        gain("hcr", D, BSP, 3)
+        gain("hcr", D, BSN, 0, False, QA)
+        plus("b2", [(0, NA, "idn", X("hcr", D, D + NA)), (0, NA, "id1", X("zz", 1024, 1024 + NA))], True)
+        act(X("mm", 3072, 3584), X("b0", 0, 512), AF.Relu)
         if r:
-            vtt(pt(1), X("ee", 0, 64), X("ee", 64, 128), OP.add)
-            vtt(pt(3), X("b7", 128, 192), X("sd", 0, 64), OP.subtract)
-            vts(pt(4), X("b7", 192, 256), 0.0, OP.is_equal, 4.0, OP.mult)
-            vtt(pt(2), X("sib", 0, 64), P_, OP.subtract)
-            vtt(pt(1), pt(0), pt(1), OP.subtract)
-            vtt(pt(6), pt(3), pt(4), OP.is_equal)
-        vtt(X("qm", 0, 128), X("q1s", 0, 128), X("b5", 0, 128), OP.max)
-        vtt(X("qq", 0, 128), X("b4", 0, 128), X("qm", 0, 128), OP.add)
-        vtt(X("ghi", 0, 64), X("qq", 0, 64), X("qq", 64, 128), OP.max)
-        vtt(X("ga", 0, 64), X("qq", 0, 64), X("qq", 64, 128), OP.max)
-        vtt(X("glo", 0, 64), X("ga", 0, 64), X("ghi", 0, 64), OP.subtract)
-        for part, buf in ((0, "ghi"), (1, "glo")):
-            for h in range(2):
-                spread1(("b0", "b1"), h, [(part, buf, 0)], False, part == 1)
-        if not last:
-            spread1(("b2", "b3"), 0, [(3, "CK", 64), (4, "CK", 192)], True, False)
+            parent_parts(False)
+        gain("mm", 1024, BSN, 1)
+        act(X("mm", 3584, 4096), X("b1", 0, 512), AF.Relu)
+        act(X("mm", 0, NA), X("b2", 0, NA), AF.Relu)
+        gain("mm", 2048, BSN, 2)
+        gain("mm", 3072, BSN, 3)
+        gain("mm", 0, BSN, 0, True)
         if r:
-            vtt(pt(2), pt(1), pt(2), OP.mult)
-            vtt(pt(6), pt(6), X("GPs", 0, 64), OP.mult)
-            vtt(pt(5), P_, pt(2), OP.add)
-            vtt(P_, pt(5), pt(6), OP.add)
-            vts(X("CKP", 0, 64), P_, 0.0625, OP.mult, 128.53125, OP.add)
-            full("b7", 320, [("id32", "PI", 0), ("idn16", "CKP", 0)], 64)
-            full("b7", 384, [("id32", "PI", 0)] + OWN, 64)
-        vts(X("gi", 0, 64), X("ga", 0, 64), 0.375, OP.add)
-        vtt(X("cd", 0, 64), X("gi", 0, 64), X("ga", 0, 64), OP.subtract)
-        if not last:
-            spread1(("b2", "b3"), 1, [(3, "CK", 64), (4, "CK", 192)], True, False)
-        if r:
-            vts(X("CKP", 64, 128), X("b7", 320, 384), 2064.0, OP.add)
-            full("b7", 320, [("id1", "CKP", 0), ("id64", "CKP", 64)], 64)
-        vts(X("cc", 0, 64), X("cd", 0, 64), 4.0, OP.mult, 1.0, OP.add)
-        act(X("GW", 0, 512), X("b0", 0, 512))
+            vcopy(lists(KL, 2), X("b5", 0, 128))
+        vcopy(lists(PAR), X("b6", 64, 128))
+        emit("V", [lambda: g.vector.tensor_tensor_scan(T.gq[:, :], T.msk[:, :], T.b4[:, 0:256], 0.0, OP.mult, OP.max)],
+             [X("msk", 0, 256), X("b4", 0, 256)], [X("gq", 0, 256)])
+        vcopy(part("XG", 0), GA)
+        vtt(part("XG", 1), GA, part("XG", 0), OP.subtract)
+        spread("XG", 0)
         if not r:
-            vcopy(X("GW", 512, 1024), X("b1", 0, 512))
-        else:
-            act(X("GW", 512, 1024), X("b1", 0, 512))
-            vts(X("PB", 0, 64), X("b7", 320, 384), -129.0, OP.add)
+            aslist("b6", 0, (PAR,), True)
+        spread("XG", 1)
+        vts(X("gi", 0, 64), GA, 0.375, OP.add)
+        vtt(part("XC", 1), X("gi", 0, 64), GA, OP.subtract)
+        vts(X("PB", 0, 64), X("b6", 0, 64), 2048.0 + D, OP.add)
+        act(X("GW", D, D + 512), X("b0", 0, 512))
+        vcopy(X("GW", D + 512, OWN), X("b1", 0, 512))
         gwin = X("GW", 0, WIN)
+        for bank, s in (("b5", 0), ("b6", 1)):
+            plus(bank, [(0, 64, "idh", X("TB", 64 * s, 64 * s + 64)), (0, 64, "idh", ONE),
+                        (64, 64, "idn", lists(KR - s)), (128, 64, "idn", lists(KR - s))])
+        plus("b7", [(0, 64, "ide", part("XG", 0)), (0, 64, "ide", part("XG", 1)), (0, 64, "ide", part("XC", 1)),
+                    (0, 64, "idf", X("TB", 128, 192)), (0, 64, "idf", ONE),
+                    (128, 128, "idn", lists(KL, 2)), (256, 128, "idk", X("ones", 0, 128))]
+             + [(oc, 64, "idn", NID) for oc in range(64, 384, 64)] + [(oc, 64, "idn", lists(PAR)) for oc in (256, 320, 384)])
+        if not r:
+            act(X("WC", 32, 40), X("OC", 0, 8), scale=-0.5)
 
-        def gather(buf, lst, o, a, b, eng):
-            eng(X(buf, a, b), ind(gwin, X(lst, o + a // 16, o + b // 16)))
+        def both(buf, w, lst, o, cut):
+            act(X(buf, 0, cut), ind(w, X(lst, o, o + cut // 16)))
+            vcopy(X(buf, cut, 1024), ind(w, X(lst, o + cut // 16, o + 64)))
 
-        def xx(oc, strip, row, side):
-            wrap("b7", oc, strip, row, plus=[("idn16", "CK", 64 * side), ("idn", "CK", 128 + 64 * side)])
-
-        gather("gl", "KB", 0, 0, 512, act)
-        gather("gr", "KB", 64, 0, 512, act)
+        both("gl", gwin, "KU", 0, 512)
+        both("gr", gwin, "KU", 64, 512)
+        both("gp", gwin, "PB", 0, 512)
+        wrap("b5", 0, "gl", 0, X("WP", 0, 24), True)
+        wrap("b6", 0, "gr", 0, X("WP", 0, 24), True)
+        wrap("b7", 0, "gp", 0, X("WG", 0, 56), True)
+        vts(X("ee", 0, 64), X("b5", 0, 64), 1.0, OP.max)
+        vtt(X("ee", 64, 128), X("b6", 0, 64), X("ee", 0, 64), OP.max)
+        vtt(X("ee", 128, 192), X("ee", 64, 128), X("gi", 0, 64), OP.is_gt)
+        vtt(part("XC", 0), X("b7", 0, 64), X("ee", 128, 192), OP.is_ge)
+        vts(part("XC", 2), X("b7", 64, 128), 0.0, OP.is_equal)
+        spread("XC", 0)
+        spread("XC", 1)
         if not last:
-            for h in range(2):
-                spread1(("b2", "b3"), h, [(1, "CKP", 0), (2, "CKP", 64)], False, False)
-        gather("gl", "KB", 0, 512, 1024, vcopy)
-        gather("gr", "KB", 64, 512, 1024, vcopy)
-        wrap("b4", 0, "sG", "gl", plus=[("idh", "TB", 0), TIE])
-        wrap("b5", 0, "sG", "gr", plus=[("idh", "TB", 64), TIE])
-        gather("gp", "PB", 0, 512, 1024, vcopy)
-        if r:
-            act(X("TB", 128, 192), X("b7", 384, 448), AF.Sign)
-        gather("gp", "PB", 0, 0, 512, act)
-        vts(X("tt", 0, 64), X("b4", 0, 64), 1.0, OP.max)
-        vtt(X("tt", 64, 128), X("b5", 0, 64), X("tt", 0, 64), OP.max)
-        wrap("b6", 0, "sG", "gp", plus=[("idh", "TB", 128), TIE])
-        xx(64, "sL", "gl", 1)
-        xx(192, "sR", "gl", 1)
-        vtt(X("tt", 128, 192), X("b6", 0, 64), X("tt", 64, 128), OP.max)
-        vtt(X("rot", 0, 64), X("gi", 0, 64), X("tt", 128, 192), OP.is_ge)
-        vtt(X("code", 0, 64), X("rot", 0, 64), X("cc", 0, 64), OP.mult)
-        if last:
-            act(X("OH", I, I + V0), X("y1", 0, V0), AF.Relu, -1.0, 255.0)
-            dma("S", T.yh[:, I:I + V0], T.OH[:, I:I + V0], [X("OH", I, I + V0)], [])
-        else:
-            act(X(nxt, I, 2049), X("y1", 0, 1025), AF.Relu, -1.0, 255.0)
-        for h in range(2):
-            spread1(("b2", "b3"), h, [(0, "code", 0)], last, True)
-        xx(0, "sL", "gr", 0)
-        xx(128, "sR", "gr", 0)
-        wrap("b6", 320, "sR", "gp", plus=[("idn16", "k129", 0)] + OWN)
-        wrap("b6", 256, "sS", "gp", plus=[("idn16", "k129", 0), ("idn16", "k129", 0)] + OWN)
-        for j, c in enumerate((3, 1, 4, 2)):
-            vts(X("MK", 64 * j, 64 * j + 64), X("code", 0, 64), float(c), OP.is_equal)
-        act(X("CW", 0, 512), X("b2", 0, 512))
-        vcopy(X("CW", 512, 1024), X("b3", 0, 512))
+            pe("b4", [(T.b4[:, 256:320], T.sPP[:, 16 - k:144 - k], T.gp[:, k:1024:16]) for k in range(16)],
+               [X("sPP", 0, 144), X("gp", 0, 1024)], True)
+        vtt(X("cod", 0, 64), part("XC", 1), part("XC", 0), OP.subtract)
+        for j in range(4):
+            vts(X("MK", 64 * j, 64 * j + 64), X("cod", 0, 64), 0.25 * j - 1.0, OP.is_equal)
+        vtt(lists(P0, 2), X("b5", 64, 192), X("MK", 0, 128), OP.mult)
+        vtt(lists(P2, 2), X("b6", 64, 192), X("MK", 128, 256), OP.mult)
+        act(X("CW", D, D + 512), X("b0", 0, 512))
+        vcopy(X("CW", D + 512, OWN), X("b1", 0, 512))
         cwin = X("CW", 0, WIN)
-        vcopy(X("cp", 768, 1024), ind(cwin, X("PB", 48, 64)))
-        act(X("cp", 0, 768), ind(cwin, X("PB", 0, 48)))
-        vtt(X("pr", 0, 256), X("b7", 0, 256), X("MK", 0, 256), OP.mult)
-        wrap("b5", 0, "sC", "cp", plus=[("idn", "ones", 0)])
+        SIDE = part("XC", 2)
+        plus("b2", [(0, 128, "idq", X("CE", 0, 128)), (0, 64, "idhn", SIDE), (64, 64, "idhn", SIDE)])
         if not last:
-            wrap("b4", 0, "sPB", "cp")
-            wrap("b4", 64, "sPn", "cp", plus=[("idn16", "CKP", 0), ("idn", "CKP", 64)])
-        vtt(X("xs", 0, 128), X("pr", 0, 128), X("pr", 128, 256), OP.add)
-        vtt(X("K1", 0, 128), X("KF", 0, 128), X("xs", 0, 128), OP.add)
-        vts(X("sd", 0, 64), X("b6", 320, 384), 0.0, OP.is_equal, 2.0, OP.mult)
-        vts(X("sd", 64, 128), X("sd", 0, 64), 1.0, OP.add)
-        vtt(X("dS", 0, 64), X("b6", 256, 320), X("KF", 0, 64), OP.subtract)
-        vtt(X("dS", 64, 128), X("b6", 256, 320), X("KF", 64, 128), OP.subtract)
-        vtt(X("ee", 0, 64), X("b5", 0, 64), X("sd", 0, 64), OP.is_equal)
-        vtt(X("ee", 64, 128), X("b5", 0, 64), X("sd", 64, 128), OP.is_equal)
-        vtt(X("te", 0, 128), X("ee", 0, 128), X("dS", 0, 128), OP.mult)
+            vts(X("PPu", 0, 64), X("b4", 256, 320), 2048.0 + D, OP.add)
+        both("cp", cwin, "PB", 0, 512)
+        aslist("b4", 0, (KL, P2, P3))
+        aslist("b4", 64, (KR, P0, P1))
         if not last:
-            vts(X("PPu", 0, 64), X("b4", 0, 64), -129.0, OP.add)
-            act(X("sib", 0, 64), X("b6", 256, 320))
-            act(X("GPs", 0, 64), X("b4", 64, 128))
-            act(X("sp", 0, 64), X("b5", 0, 64), AF.Sign, 1.0, 0.5)
-            act(pt(0), X("sp", 0, 64), AF.Relu)
-        vtt(X("KF", 0, 128), X("K1", 0, 128), X("te", 0, 128), OP.add)
-        vcopy(X("KU", 0, 128), X("KF", 0, 128))
+            plus("b3", [(0, 128, "idq", X("CE", 128, 256)), (128, 64, "id1", ONE), (0, 64, "idh", SIDE), (64, 64, "idh", SIDE), (128, 64, "idq", SIDE)])
+        wrap("b2", 0, "cp", 0, X("WC", 0, 16), True)
+        if not last:
+            act(X("cg", 0, 1024), ind(cwin, X("PPu", 0, 64)))
+            wrap("b3", 0, "cp", 0, X("WC", 16, 40))
+        vts(X("E1", 0, 128), X("b2", 0, 128), 0.0, OP.is_equal)
+        vtt(lists(TL, 2), X("b7", 128, 256), X("E1", 0, 128), OP.mult)
+        aslist("b4", 0, (TL,))
+        aslist("b4", 64, (TR,), True)
+        children(0, False, last)
+        vts(X("KU", 0, 128), X("b4", 0, 128), float(D), OP.add)
         if last:
-            act(X("fh", 0, 128), X("KF", 0, 128))
-            vtt(X("fl", 0, 128), X("KF", 0, 128), X("fh", 0, 128), OP.subtract)
-        act(X("rr", 0, 320), ind(win, X("KU", 64, 84)))
-        act(X("rr", 320, 640), ind(win, X("KU", 84, 104)))
-        vcopy(X("rr", 640, 1024), ind(win, X("KU", 104, 128)))
+            vcopy(lists(KL, 2), X("b5", 0, 128))
+            for h in range(2):
+                pe("b%d" % h, [(T["b%d" % h][0:16, b:512:8], T.L[:, 1:33:2, b], T.id1[:, 8 * h:8 * h + 8, :]) for b in range(8)],
+                   [lists(KL, 2), ID], True)
+        cuts = (0, 256, 512, 768, 1024)
+        vcopy(X("rr", 0, 256), ind(win, X("KU", 64, 80)))
+        for a, b in zip(cuts[1:], cuts[2:]):
+            act(X("rr", a, b), ind(win, X("KU", 64 + a // 16, 64 + b // 16)))
         if not last:
-            chunks()
-            act(X("cg", 0, 512), ind(cwin, X("PPu", 0, 32)))
-            act(X("CK", 128, 256), X("b4", 128, 256), scale=1.0, bias=2064.0)
-            act(X("cg", 512, 1024), ind(cwin, X("PPu", 32, 64)))
-        dst = "OH" if last else nxt
-        for a, b in ((640, 1024), (0, 320), (320, 640)):
-            vtt(X(dst, a, b), ind(win, X("KU", a // 16, b // 16)), X("rr", a, b), OP.max)
+            wrap("b3", 128, "cg", 0, X("WC", 0, 8), True)
+            child_parts(False)
+        for a, b in zip(cuts, cuts[1:]):
+            vtt(X("OH", a, b) if last else X("H%d" % (r + 1), D + a, D + b), ind(win, X("KU", a // 16, b // 16)), X("rr", a, b), OP.max)
             if last:
                 dma("S", T.yh[:, a:b], T.OH[:, a:b], [X("OH", a, b)], [])
-        cur, nxt = nxt, cur
 
-    for b in range(4):
-        bank = "b%d" % b
-        o = X("OK", 512 * b, 512 * b + 512)
-        fns = []
-        for j, buf in enumerate(("fh", "fl")):
-            for k in range(16):
-                fns.append(mm(T[bank][0:8, k:512:16], T.idp[:, 8 * k:8 * k + 8], T[buf][:, 32 * b:32 * b + 32],
-                              j == 0 and k == 0, j == 1 and k == 15))
-        emit("P", fns, [X("idp", 0, 128), X("fh", 0, 128), X("fl", 0, 128)], [X(bank, 0, 512)])
-        emit("A", [lambda: g.scalar.activation(T.OK[0:8, 512 * b:512 * b + 512], T[bank][0:8, 0:512], AF.Copy)],
-             [X(bank, 0, 512)], [o])
-        dma("S", T.yk[:, 512 * b:512 * b + 512], T.OK[0:8, 512 * b:512 * b + 512], [o], [])
+    for h in range(2):
+        o = X("OK", 512 * h, 512 * h + 512)
+        emit("A", [lambda: g.scalar.activation(T.OK[0:16, 512 * h:512 * h + 512], T["b%d" % h][0:16, 0:512], AF.Copy)],
+             [X("b%d" % h, 0, 512)], [o])
+    for s in range(2):
+        dma("A", T.yk[:, 1024 * s:1024 * s + 1024], T.OK[8 * s:8 * s + 8, :], [X("OK", 0, 1024)], [])
     cnt["sent"] = nsent[0]
     for s, c in cnt.items():
         g.wait_ge(T.sem[s], c)

@@ -9,6 +9,9 @@ OWN, GHO, WIN = I + D, I + V0 + D, 2049 + D
 KL, KR, P2, P3, P0, P1, TL, TR, PAR, W0, W1, XX = range(12)
 QA = 64
 
+CG = 704
+CUTS = (0, 128, 384, 704, 1024)
+
 SCRATCH = {"b%d" % _b: ("psum", [128, 512], "float32") for _b in range(8)}
 for _dt, _names in (
         ("int32", "hl 360 hi 1024 vi 360 si 48 KI 128 gi 64"),
@@ -16,7 +19,7 @@ for _dt, _names in (
         ("float16", "KW 272 nid 320"),
         ("bfloat16", "H0 2064 H1 2064 H2 2064 vo 368 s0 672 s1 672 s2 672 hcl 2064 hcr 2064 hr2 1024 mm 4096 zz 2048 rr 1024 "
                      "GW 2064 CW 2064 PW 2064 nrow 1024 gl 1024 gr 1024 gp 1024 cp 1024 cg 1024 ones 128 idn 128 idh 128 idhn 128 "
-                     "idq 128 ide 128 idf 128 idk 128 WP 32 WG 56 OC 24 WC 40 BS 16 sPP 144 CQ 256 CE 320 msk 256 TB 192 "
+                     "idq 128 ide 128 idf 128 idk 128 WP 32 WG 56 WR 24 OC 24 WC 40 BS 16 sPP 144 CQ 256 CE 320 msk 256 TB 192 "
                      "cod 64 MK 256 E1 128 E2 192"),
         ("float32", "nf 64 gq 256 ee 192 y1 360 OK 1024 OH 1384")):
     _w = _names.split()
@@ -219,7 +222,6 @@ def rank_program(g, core, T, topo):
     gsel(X("BS", 0, 8), X("BS", 0, 8), [[16, 8]], OP.is_ge, 15, -1)
     for nm in ("H0", "H1", "H2", "hcl", "hcr", "GW", "CW"):
         giota(X(nm, 0, D), [[0, D]], 0, 0)
-    emit("V", [lambda: g.vector.memset(T.XG[:], 0.0)], [], [(None, "XG", 0, 16)])
     act(X("nrow", 0, 512), X("b0", 0, 512))
     act(X("nrow", 512, 1024), X("b1", 0, 512))
     vts(X("su", 0, 42), X("si", 0, 42), float(D), OP.add)
@@ -255,11 +257,13 @@ def rank_program(g, core, T, topo):
     scatter(0)
     for s in range(2):
         vcopy(X("KW", 136 * s + 1, 136 * s + 129, 2), X("KI", 64 * s, 64 * s + 64))
-    vts(X("nid", 0, 64), X("nf", 0, 64), 2048.0, OP.add)
+    for j in range(2):
+        vts(X("nid", 64 * j, 64 * j + 64), X("nf", 0, 64), 2048.0, OP.add)
     scatter(64)
-    for nm, w in (("idn", -1.0), ("idh", 0.5), ("idhn", -0.5), ("idq", -0.25), ("ide", 2.0 ** -13), ("idf", -2.0 ** -14),
+    for nm, w in (("idn", -1.0), ("idh", 0.5), ("idhn", -0.5), ("idq", -0.25), ("ide", 2.0 ** -13), ("idf", -2.0 ** -13),
                   ("idk", -2048.0)):
         act(X(nm, 0, 128), ID, scale=w)
+    act((T.XG[:], "XG", 0, 16), X("nrow", 0, 1024), scale=0.0)
     for nm in ("hcl", "hcr"):
         act(X(nm, OWN, OWN + 1024), X("nrow", 0, 1024), scale=0.0, bias=255.0)
         act(X(nm, WIN - 1, WIN), X("nrow", 0, 1), scale=0.0, bias=255.0)
@@ -269,15 +273,14 @@ def rank_program(g, core, T, topo):
         act(X("y1", 0, V0), X("b2", 0, V0), AF.Relu, scale=-1.0, bias=255.0)
         act(X("OH", I, I + V0) if r == RO - 1 else X("H%d" % (r + 1), OWN, GHO), X("y1", 0, V0), AF.Relu, scale=-1.0, bias=255.0)
 
-    for r in range(1, RO):
-        leaves(r - 1)
+    def ghosts(r):
         act(X("s%d" % r, 0, 672), ind(X("H%d" % r, I, GHO), X("su", 0, 42)))
-        if r == 1:
-            giota(X("CQ", 0, 256), [[0, 64], [1, 4]], 0, 0)
         exchange(r)
-        giota(X("GW" if r == 1 else "CW", OWN, WIN), [[0, WIN - OWN]], 0, 0)
-    leaves(RO - 1)
-    dma("S", T.yh[:, I:I + V0], T.OH[:, I:I + V0], [X("OH", I, I + V0)], [])
+
+    leaves(0)
+    giota(X("CQ", 0, 256), [[0, 64], [1, 4]], 0, 0)
+    ghosts(1)
+    giota(X("GW", OWN, WIN), [[0, WIN - OWN]], 0, 0)
     giota(X("CE", 0, 256), [[1, 4], [0, 64]], -4, 0)
     gsel(X("WG", 16, 48), X("ones", 0, 32), [[0, 4], [-16, 8]], OP.is_ge, -2, 1)
     gsel(X("WG", 16, 48), X("WG", 16, 48), [[0, 4], [16, 8]], OP.is_ge, 5, -1)
@@ -289,54 +292,26 @@ def rank_program(g, core, T, topo):
     NID = X("nid", 0, 64)
     ONE = X("ones", 0, 64)
 
-    def children(oc, first, last):
-        if first:
-            pe("b5", [(T.b5[:, oc + 64 * s:oc + 64 * s + 64], T.KW[:, 136 * s + 1 - h:136 * s + 129 - h], T.id1[:, h::2, :])
-                      for s in range(2) for h in range(2)], [X("KW", 0, 272), ID], last)
-        else:
-            plus("b5", [(oc, 128, "id1", lists(KL, 2)), (oc, 64, "id1", lists(P2)), (oc, 64, "id1", lists(P3)),
-                        (oc + 64, 64, "id1", lists(P0)), (oc + 64, 64, "id1", lists(P1)), (oc, 128, "id1", lists(TL, 2))], last)
+    def rounded(p, bank, oc):
+        act(part("XG", p), X(bank, oc, oc + 64))
 
-    def child_parts(first):
-        children(128, first, False)
-        plus("b5", [(128, 64, "idn", NID), (192, 64, "idn", NID)], True)
-        act(part("XG", 2), X("b5", 0, 64))
-        act(part("XG", 4), X("b5", 64, 128))
-        act(X("TB", 0, 128), X("b5", 128, 256), AF.Sign)
-        children(256, first, False)
-        plus("b5", [(256, 64, "idn", part("XG", 2)), (320, 64, "idn", part("XG", 4))], True)
-        act(part("XG", 3), X("b5", 256, 320))
-        act(part("XG", 5), X("b5", 320, 384))
+    def rest(p, bank, oc):
+        vtt(part("XG", p + 1), X(bank, oc, oc + 64), part("XG", p), OP.subtract)
 
-    def parents(oc, first):
-        if first:
-            wrap("b6", oc, "PW", D, X("WP", 0, 8))
-        else:
-            plus("b6", [(oc, 64, "id1", lists(a)) for a in (PAR, W0, W1, XX)])
-
-    def parent_parts(first):
-        parents(64, first)
-        parents(128, first)
-        if not first:
-            aslist("b6", 0, (PAR, W0, W1, XX))
-        plus("b6", [(128, 64, "idn", NID)], True)
-        act(part("XG", 6), X("b6", 64, 128))
-        act(X("TB", 128, 192), X("b6", 128, 192), AF.Sign, bias=2048.0)
-        parents(192, first)
-        plus("b6", [(192, 64, "idn", part("XG", 6))], True)
-        act(part("XG", 7), X("b6", 192, 256))
-
-    children(0, True, False)
-    child_parts(True)
+    pe("b5", [(T.b5[:, 64 * s:64 * s + 64], T.KW[:, 136 * s + 1 - h:136 * s + 129 - h], T.id1[:, h::2, :])
+              for s in range(2) for h in range(2)], [X("KW", 0, 272), ID], True)
+    rounded(2, "b5", 0)
+    rounded(4, "b5", 64)
     act(X("BS", 8, 16), X("BS", 0, 8), scale=-1.0)
     act(X("msk", 0, 256), X("CQ", 0, 256), AF.Sign)
-    parent_parts(True)
-    act(X("WG", 0, 8), X("WP", 0, 8), scale=-2.0 ** -13)
+    act(X("WG", 0, 8), X("WP", 0, 8))
     act(X("WG", 8, 16), X("WP", 16, 24))
     act(X("WG", 48, 56), X("WP", 24, 32))
-    vcopy(lists(KL, 2), X("b5", 0, 128))
-    vset(X("sPP", 0, 144), 0.0)
-    vcopy(X("sPP", 16, 144, 16), X("WP", 24, 32))
+    act(X("WR", 0, 8), X("WP", 0, 8), scale=-2.0 ** -13)
+    act(X("WR", 8, 24), X("WP", 8, 24))
+    act(X("sPP", 0, 144), X("nrow", 0, 144), scale=0.0)
+    act(X("sPP", 16, 144, 16), X("WP", 24, 32))
+    wrap("b6", 64, "PW", D, X("WP", 0, 8), True)
 
     BSP, BSN = X("BS", 0, 8), X("BS", 8, 16)
     GA = X("gq", 3, 256, 4)
@@ -354,7 +329,9 @@ def rank_program(g, core, T, topo):
         if r:
             vts(X("E2", 0, 192), X("b3", 0, 192), 0.0, OP.is_equal)
             vtt(lists(W0, 3), X("b7", 256, 448), X("E2", 0, 192), OP.mult)
-        vcopy(X("hr2", NA, 1024), X("hcr", D + NA, OWN))
+        gsel(X("hr2", NA, 1024), X("hcr", D + NA, OWN), [[0, 1024 - NA]], OP.is_ge, 0, 0)
+        if not r:
+            giota(X("CW", OWN, WIN), [[0, WIN - OWN]], 0, 0)
         plus("b4", [(0, 256, "idq", X("CQ", 0, 256))])
         act(X("zz", 0, 512), ind(wl, X("KU", 64, 96)))
         act(X("zz", 512, 1024), ind(wl, X("KU", 96, 128)))
@@ -366,44 +343,57 @@ def rank_program(g, core, T, topo):
         gain("hcl", D, BSP, 1)
         plus("b0", [(0, 512, "idn", X("hcl", D, D + 512)), (0, 512, "id1", X("zz", 0, 512))], True)
         gain("hcl", D, BSN, 3)
+        if r:
+            plus("b6", [(64, 64, "id1", lists(a)) for a in (PAR, W0, W1, XX)])
+            aslist("b6", 0, (PAR, W0, W1, XX), True)
+        plus("b3", [(0, 512, "idn", X("hcl", D + 512, OWN)), (0, 512, "id1", X("zz", 512, 1024))], True)
         gain("hcr", D, BSP, 2)
-        plus("b1", [(0, 512, "idn", X("hcl", D + 512, OWN)), (0, 512, "id1", X("zz", 512, 1024))], True)
         gain("hcr", D, BSP, 3)
         gain("hcr", D, BSN, 0, False, QA)
         plus("b2", [(0, NA, "idn", X("hcr", D, D + NA)), (0, NA, "id1", X("zz", 1024, 1024 + NA))], True)
+        if not last:
+            rounded(6, "b6", 64)
         act(X("mm", 3072, 3584), X("b0", 0, 512), AF.Relu)
-        if r:
-            parent_parts(False)
         gain("mm", 1024, BSN, 1)
-        act(X("mm", 3584, 4096), X("b1", 0, 512), AF.Relu)
+        act(X("mm", 3584, 4096), X("b3", 0, 512), AF.Relu)
         act(X("mm", 0, NA), X("b2", 0, NA), AF.Relu)
         gain("mm", 2048, BSN, 2)
         gain("mm", 3072, BSN, 3)
         gain("mm", 0, BSN, 0, True)
-        if r:
-            vcopy(lists(KL, 2), X("b5", 0, 128))
-        vcopy(lists(PAR), X("b6", 64, 128))
+        if r < 2:
+            leaves(r + 1)
+        if r == 1:
+            dma("S", T.yh[:, I:I + V0], T.OH[:, I:I + V0], [X("OH", I, I + V0)], [])
+        rest(2, "b5", 0)
+        rest(4, "b5", 64)
+        vcopy(lists(KL, 2), X("b5", 0, 128))
+        if not last:
+            rest(6, "b6", 64)
+            vcopy(lists(PAR), X("b6", 64, 128))
         emit("V", [lambda: g.vector.tensor_tensor_scan(T.gq[:, :], T.msk[:, :], T.b4[:, 0:256], 0.0, OP.mult, OP.max)],
              [X("msk", 0, 256), X("b4", 0, 256)], [X("gq", 0, 256)])
         vcopy(part("XG", 0), GA)
         vtt(part("XG", 1), GA, part("XG", 0), OP.subtract)
-        spread("XG", 0)
         if not r:
             aslist("b6", 0, (PAR,), True)
+        spread("XG", 0)
         spread("XG", 1)
+        vtt(X("TB", 128, 192), X("b6", 64, 128), X("nf", 0, 64), OP.is_gt)
+        vts(X("PB", 0, 64), X("b6", 0, 64), 2048.0 + D, OP.add)
+        vtt(X("TB", 0, 128), X("b5", 0, 128), X("nid", 0, 128), OP.is_gt)
         vts(X("gi", 0, 64), GA, 0.375, OP.add)
         vtt(part("XC", 1), X("gi", 0, 64), GA, OP.subtract)
-        vts(X("PB", 0, 64), X("b6", 0, 64), 2048.0 + D, OP.add)
         act(X("GW", D, D + 512), X("b0", 0, 512))
         vcopy(X("GW", D + 512, OWN), X("b1", 0, 512))
         gwin = X("GW", 0, WIN)
-        for bank, s in (("b5", 0), ("b6", 1)):
-            plus(bank, [(0, 64, "idh", X("TB", 64 * s, 64 * s + 64)), (0, 64, "idh", ONE),
-                        (64, 64, "idn", lists(KR - s)), (128, 64, "idn", lists(KR - s))])
-        plus("b7", [(0, 64, "ide", part("XG", 0)), (0, 64, "ide", part("XG", 1)), (0, 64, "ide", part("XC", 1)),
-                    (0, 64, "idf", X("TB", 128, 192)), (0, 64, "idf", ONE),
-                    (128, 128, "idn", lists(KL, 2)), (256, 128, "idk", X("ones", 0, 128))]
-             + [(oc, 64, "idn", NID) for oc in range(64, 384, 64)] + [(oc, 64, "idn", lists(PAR)) for oc in (256, 320, 384)])
+        plus("b7", [(0, 64, "id1", X("TB", 128, 192)), (128, 128, "idn", lists(KL, 2)), (64, 64, "idn", NID),
+                    (128, 128, "idn", X("nid", 0, 128))])
+        if not last:
+            plus("b7", [(256, 128, "idk", X("ones", 0, 128)), (256, 128, "idn", X("nid", 0, 128))]
+                 + [(oc, 64, "idn", lists(PAR)) for oc in (256, 320, 384)])
+        plus("b5", [(0, 64, "id1", X("TB", 0, 64)), (64, 64, "idn", lists(KR)), (128, 64, "idn", lists(KR))])
+        plus("b6", [(0, 64, "ide", part("XG", 0)), (0, 64, "ide", part("XG", 1)), (0, 64, "ide", part("XC", 1)),
+                    (0, 64, "idf", X("TB", 64, 128)), (64, 64, "idn", lists(KL)), (128, 64, "idn", lists(KL))])
         if not r:
             act(X("WC", 32, 40), X("OC", 0, 8), scale=-0.5)
 
@@ -411,72 +401,79 @@ def rank_program(g, core, T, topo):
             act(X(buf, 0, cut), ind(w, X(lst, o, o + cut // 16)))
             vcopy(X(buf, cut, 1024), ind(w, X(lst, o + cut // 16, o + 64)))
 
+        both("gp", gwin, "PB", 0, 512)
         both("gl", gwin, "KU", 0, 512)
         both("gr", gwin, "KU", 64, 512)
-        both("gp", gwin, "PB", 0, 512)
-        wrap("b5", 0, "gl", 0, X("WP", 0, 24), True)
-        wrap("b6", 0, "gr", 0, X("WP", 0, 24), True)
-        wrap("b7", 0, "gp", 0, X("WG", 0, 56), True)
-        vts(X("ee", 0, 64), X("b5", 0, 64), 1.0, OP.max)
-        vtt(X("ee", 64, 128), X("b6", 0, 64), X("ee", 0, 64), OP.max)
-        vtt(X("ee", 128, 192), X("ee", 64, 128), X("gi", 0, 64), OP.is_gt)
-        vtt(part("XC", 0), X("b7", 0, 64), X("ee", 128, 192), OP.is_ge)
-        vts(part("XC", 2), X("b7", 64, 128), 0.0, OP.is_equal)
-        spread("XC", 0)
-        spread("XC", 1)
+        wrap("b7", 0, "gp", 0, X("WG", 0, 32 if last else 56), True)
         if not last:
             pe("b4", [(T.b4[:, 256:320], T.sPP[:, 16 - k:144 - k], T.gp[:, k:1024:16]) for k in range(16)],
                [X("sPP", 0, 144), X("gp", 0, 1024)], True)
+        wrap("b5", 0, "gl", 0, X("WP", 0, 24), True)
+        wrap("b6", 0, "gr", 0, X("WR", 0, 24), True)
+        if not r:
+            ghosts(2)
+        vts(X("ee", 0, 64), X("b7", 0, 64), 1.0, OP.max)
+        vts(part("XC", 2), X("b7", 64, 128), 0.0, OP.is_equal)
+        vtt(X("ee", 64, 128), X("b5", 0, 64), X("ee", 0, 64), OP.max)
+        if not last:
+            vts(X("PPu", 0, 64), X("b4", 256, 320), 2048.0 + D, OP.add)
+        vtt(X("ee", 128, 192), X("ee", 64, 128), X("gi", 0, 64), OP.is_gt)
+        vtt(part("XC", 0), X("b6", 0, 64), X("ee", 128, 192), OP.is_ge)
+        spread("XC", 0)
+        spread("XC", 1)
         vtt(X("cod", 0, 64), part("XC", 1), part("XC", 0), OP.subtract)
         for j in range(4):
             vts(X("MK", 64 * j, 64 * j + 64), X("cod", 0, 64), 0.25 * j - 1.0, OP.is_equal)
-        vtt(lists(P0, 2), X("b5", 64, 192), X("MK", 0, 128), OP.mult)
-        vtt(lists(P2, 2), X("b6", 64, 192), X("MK", 128, 256), OP.mult)
         act(X("CW", D, D + 512), X("b0", 0, 512))
         vcopy(X("CW", D + 512, OWN), X("b1", 0, 512))
         cwin = X("CW", 0, WIN)
         SIDE = part("XC", 2)
         plus("b2", [(0, 128, "idq", X("CE", 0, 128)), (0, 64, "idhn", SIDE), (64, 64, "idhn", SIDE)])
-        if not last:
-            vts(X("PPu", 0, 64), X("b4", 256, 320), 2048.0 + D, OP.add)
         both("cp", cwin, "PB", 0, 512)
-        aslist("b4", 0, (KL, P2, P3))
-        aslist("b4", 64, (KR, P0, P1))
+        aslist("b4", 0, (KL,))
+        aslist("b4", 64, (KR,))
         if not last:
-            plus("b3", [(0, 128, "idq", X("CE", 128, 256)), (128, 64, "id1", ONE), (0, 64, "idh", SIDE), (64, 64, "idh", SIDE), (128, 64, "idq", SIDE)])
+            plus("b3", [(0, 128, "idq", X("CE", 128, 256)), (128, 64, "id1", ONE), (0, 64, "idh", SIDE), (64, 64, "idh", SIDE),
+                        (128, 64, "idq", SIDE)])
         wrap("b2", 0, "cp", 0, X("WC", 0, 16), True)
+        vtt(lists(P0, 2), X("b5", 64, 192), X("MK", 0, 128), OP.mult)
+        vtt(lists(P2, 2), X("b6", 64, 192), X("MK", 128, 256), OP.mult)
+        aslist("b4", 64, (P0, P1))
+        aslist("b4", 0, (P2, P3))
         if not last:
-            act(X("cg", 0, 1024), ind(cwin, X("PPu", 0, 64)))
-            wrap("b3", 0, "cp", 0, X("WC", 16, 40))
+            act(X("cg", 0, CG), ind(cwin, X("PPu", 0, CG // 16)))
         vts(X("E1", 0, 128), X("b2", 0, 128), 0.0, OP.is_equal)
         vtt(lists(TL, 2), X("b7", 128, 256), X("E1", 0, 128), OP.mult)
         aslist("b4", 0, (TL,))
         aslist("b4", 64, (TR,), True)
-        children(0, False, last)
+        plus("b5", [(0, 128, "id1", lists(KL, 2)), (0, 64, "id1", lists(P2)), (0, 64, "id1", lists(P3)),
+                    (64, 64, "id1", lists(P0)), (64, 64, "id1", lists(P1)), (0, 128, "id1", lists(TL, 2))], True)
         vts(X("KU", 0, 128), X("b4", 0, 128), float(D), OP.add)
+        cuts = (0, 128, 448, 768, 1024) if last else CUTS
         if last:
             vcopy(lists(KL, 2), X("b5", 0, 128))
             for h in range(2):
-                pe("b%d" % h, [(T["b%d" % h][0:16, b:512:8], T.L[:, 1:33:2, b], T.id1[:, 8 * h:8 * h + 8, :]) for b in range(8)],
-                   [lists(KL, 2), ID], True)
-        cuts = (0, 256, 512, 768, 1024)
-        vcopy(X("rr", 0, 256), ind(win, X("KU", 64, 80)))
-        for a, b in zip(cuts[1:], cuts[2:]):
-            act(X("rr", a, b), ind(win, X("KU", 64 + a // 16, 64 + b // 16)))
+                pe("b0", [(T.b0[64 * h:64 * h + 64, b:512:8], T.L[:, 1:129:2, b], T.id1[:, 8 * h:8 * h + 8, :]) for b in range(8)],
+                   [lists(KL, 8), ID], True)
+        for j, (a, b) in enumerate(zip(cuts, cuts[1:])):
+            (act if j else vcopy)(X("rr", a, b), ind(win, X("KU", 64 + a // 16, 64 + b // 16)))
+        if last:
+            act(X("OK", 0, 512), X("b0", 0, 512))
+            for h in range(2):
+                for s in range(2):
+                    dma("A", T.yk[:, 1024 * s + 512 * h:1024 * s + 512 * h + 512], T.OK[64 * h + 8 * s:64 * h + 8 * s + 8, 0:512],
+                        [X("OK", 0, 512)], [])
         if not last:
+            wrap("b3", 0, "cp", 0, X("WC", 16, 40))
+            act(X("cg", CG, 1024), ind(cwin, X("PPu", CG // 16, 64)))
             wrap("b3", 128, "cg", 0, X("WC", 0, 8), True)
-            child_parts(False)
+            rounded(2, "b5", 0)
+            rounded(4, "b5", 64)
         for a, b in zip(cuts, cuts[1:]):
             vtt(X("OH", a, b) if last else X("H%d" % (r + 1), D + a, D + b), ind(win, X("KU", a // 16, b // 16)), X("rr", a, b), OP.max)
             if last:
                 dma("S", T.yh[:, a:b], T.OH[:, a:b], [X("OH", a, b)], [])
 
-    for h in range(2):
-        o = X("OK", 512 * h, 512 * h + 512)
-        emit("A", [lambda: g.scalar.activation(T.OK[0:16, 512 * h:512 * h + 512], T["b%d" % h][0:16, 0:512], AF.Copy)],
-             [X("b%d" % h, 0, 512)], [o])
-    for s in range(2):
-        dma("A", T.yk[:, 1024 * s:1024 * s + 1024], T.OK[8 * s:8 * s + 8, :], [X("OK", 0, 1024)], [])
     cnt["sent"] = nsent[0]
     for s, c in cnt.items():
         g.wait_ge(T.sem[s], c)

@@ -7,32 +7,29 @@ I, V0, GH, RO = 1024, 353, 96, 3
 D = 7
 OWN, GHO, WIN = I + D, I + V0 + D, 2049 + D
 KL, KR, P2, P3, P0, P1, TL, TR, PAR, W0, W1, XX = range(12)
-QA = 64
-
 CG = 704
-CUTS = (0, 128, 384, 704, 1024)
+CUTS = (0, 192, 608, 1024)
 
 SCRATCH = {"b%d" % _b: ("psum", [128, 512], "float32") for _b in range(8)}
 for _dt, _names in (
         ("int32", "hl 360 hi 1024 vi 360 si 48 KI 128 gi 64"),
-        ("uint16", "su 48 KU 128 PB 64 PPu 64"),
-        ("float16", "KW 272 nid 320"),
-        ("bfloat16", "H0 2064 H1 2064 H2 2064 vo 368 s0 672 s1 672 s2 672 hcl 2064 hcr 2064 hr2 1024 mm 4096 zz 2048 rr 1024 "
-                     "GW 2064 CW 2064 PW 2064 nrow 1024 gl 1024 gr 1024 gp 1024 cp 1024 cg 1024 ones 128 idn 128 idh 128 idhn 128 "
-                     "idq 128 ide 128 idf 128 idk 128 WP 32 WG 56 WR 24 OC 24 WC 40 BS 16 sPP 144 CQ 256 CE 320 msk 256 TB 192 "
-                     "cod 64 MK 256 E1 128 E2 192"),
-        ("float32", "nf 64 gq 256 ee 192 y1 360 OK 1024 OH 1384")):
+        ("uint16", "su 48 KU 128 KC 128 PB 64 PPu 64"),
+        ("float16", "KW 272 nid 128"),
+        ("bfloat16", "H0 2064 H1 2064 H2 2064 vo 368 s0 672 s1 672 s2 672 hcl 1040 hcr 1040 hr2 1024 mm 4096 zz 2048 rr 1024 "
+                     "GW 1040 CW 1040 gl 1024 gr 1024 gp 1024 cp 1024 cg 1024 ones 128 idn 128 idh 128 idhn 128 "
+                     "idq 128 ide 128 idf 128 idk 128 WP 32 WG 56 WR 24 OC 24 WC 40 BS 64 sPP 144 CQ 256 CE 320 msk 256 TB 192 "
+                     "cd 64 cod 64 MK 256 E1 128 E2 192"),
+        ("float32", "nf 64 gq 256 ee 192 y1 360 OK 512 OH 1384 PW 2064 PA 2064 nrow 1024 O32 8")):
     _w = _names.split()
     for _n, _c in zip(_w[::2], _w[1::2]):
         SCRATCH[_n] = ("sbuf", [128, int(_c)], _dt)
 SCRATCH["L"] = ("sbuf", [128, 193, 8], "float16")
 SCRATCH["id1"] = ("sbuf", [128, 16, 8], "bfloat16")
 SCRATCH["XG"] = ("sbuf", [128, 8, 16, 8], "bfloat16")
-SCRATCH["XC"] = ("sbuf", [128, 8, 16, 8], "bfloat16")
 SEMAPHORES = ["V", "A", "P", "G", "arr0", "arr1", "arr2", "sent"] + ["d%d" % _i for _i in range(20)]
 
 
-def sends(T, topo, q):
+def sends(T, topo, q, urgent):
     src = T.cores[q]
     dst = {d: T.cores[(q + d) % 8] for d in range(1, 8)}
     near = [d for d in dst if topo.chip(dst[d]) == topo.chip(src)]
@@ -43,18 +40,19 @@ def sends(T, topo, q):
         a, b = topo.chip(src), topo.chip(dst[d])
         return topo.mates(a, b) or topo.same_plane(a, b)
     far.sort(key=lambda d: (direct(d), d))
-    out = {}
-    spare = len(pool) - len(far)
-    used = 0
-    for d in far:
-        k = 2 if spare > 0 else 1
-        spare -= k - 1
-        out[d] = pool[used:used + k]
-        used += k
-    rest = [e for e in topo.engines(src, dst[near[0]]) if e not in pool]
-    for j, d in enumerate(near):
-        out[d] = rest[j:j + 1]
-    return out
+    n = 1 << len(far).bit_length() - 1
+    rest = [e for e in topo.engines(src, dst[near[0]]) if e not in pool][:len(pool) // n]
+    if not urgent:
+        spare = len(pool) - len(far)
+        call = {d: pool[2 * j:2 * j + 2] if j < spare else pool[spare + j:spare + j + 1] for j, d in enumerate(far)}
+        call[near[0]] = rest
+        return [call]
+    calls = []
+    for ds in (far[:n], far[n:]):
+        k = len(pool) // len(ds)
+        calls.append({d: pool[k * j:k * j + k] for j, d in enumerate(ds)})
+    calls[1][near[0]] = rest
+    return calls
 
 
 def rank_program(g, core, T, topo):
@@ -151,8 +149,8 @@ def rank_program(g, core, T, topo):
     def vtt(out, a, b, op):
         emit("V", [lambda: g.vector.tensor_tensor(out[0], a[0], b[0], op)], flat(a, b), [out])
 
-    def vts(out, a, s1, op0):
-        emit("V", [lambda: g.vector.tensor_scalar(out[0], a[0], s1, None, op0)], [a], [out])
+    def vts(out, a, s1, op0, s2=None, *op1):
+        emit("V", [lambda: g.vector.tensor_scalar(out[0], a[0], s1, s2, op0, *op1)], [a], [out])
 
     def vset(out, c):
         emit("V", [lambda: g.vector.memset(out[0], c)], [], [out])
@@ -160,11 +158,15 @@ def rank_program(g, core, T, topo):
     def act(out, in_, func=AF.Copy, **kw):
         emit("A", [lambda: g.scalar.activation(out[0], in_[0], func, **kw)], flat(in_), [out])
 
-    def gsel(out, in_, pattern, op, base, cm):
-        emit("G", [lambda: g.affine_select(out[0], in_[0], pattern, op, 0.0, base, cm)], [in_], [out])
+    def gsel(out, in_, pattern, op, base, cm, fill=0.0):
+        emit("G", [lambda: g.affine_select(out[0], in_[0], pattern, op, fill, base, cm)], [in_], [out])
 
     def giota(out, pattern, base, cm):
         emit("G", [lambda: g.iota(out[0], pattern, base, cm, allow_small_or_imprecise_dtypes=True)], [], [out])
+
+    def diagonal(*names):
+        for nm, w in names:
+            gsel(X(nm, 0, 128), (T.XG[:, 0:4, 12:16, :], "XG", 12, 16), [[-1, 128]], OP.not_equal, 0, 1, w)
 
     ID = (T.id1[:, :, :], "id1", 0, 128)
     opened = set()
@@ -181,19 +183,23 @@ def rank_program(g, core, T, topo):
 
     def plus(bank, terms, last=False):
         dg = [ID if t[2] == "id1" else X(t[2], 0, 128) for t in terms]
-        pe(bank, [(T[bank][:, t[0]:t[0] + t[1]], d[0], t[3][0]) for t, d in zip(terms, dg)], dg + [t[3] for t in terms], last)
+        pe(bank, [(X(bank, t[0], t[0] + t[1])[0], d[0], t[3][0]) for t, d in zip(terms, dg)], dg + [t[3] for t in terms], last)
 
-    def wrap(bank, oc, row, off, w, last=False, step=8, at=1, nq=128):
+    def wrap(bank, oc, row, off, w, last=False):
         n = w[3] - w[2]
-        pe(bank, [(T[bank][0:nq, oc + at * b:oc + at * b + step * (n - 1) + 1:step], T[row][:, off + b:off + 8 * nq:8], w[0])
-                  for b in range(8)], [X(row, off, off + 8 * nq), w], last)
+        pe(bank, [(T[bank][:, oc + b:oc + 8 * n:8], T[row][:, off + b:off + 1024:8], w[0]) for b in range(8)],
+           [X(row, off, off + 1024), w], last)
+
+    def gain(row, off, w, ch, last=False, nq=128):
+        pe("b4", [(T.b4[0:nq, 4 * b + ch:256:32], T[row][:, off + b:off + 8 * nq:8], w[0]) for b in range(8)],
+           [X(row, off, off + 1024), w], last)
 
     def spread(buf, h):
         pe("b%d" % h, [(T["b%d" % h][:, b:512:8], T[buf][:, :, :, b], T.id1[:, 8 * h:8 * h + 8, :]) for b in range(8)],
            [(None, buf, 0, 16), ID], True)
 
     def aslist(bank, oc, which, last=False):
-        pe(bank, [(T[bank][:, oc:oc + 64], T.L[:, 16 * a + 1 - h:16 * a + 17 - h, :], T.id1[:, :, h::2]) for a in which for h in range(2)],
+        pe(bank, [(X(bank, oc, oc + 64)[0], T.L[:, 16 * a + 1 - h:16 * a + 17 - h, :], T.id1[:, :, h::2]) for a in which for h in range(2)],
            [lists(a) for a in which] + [ID], last)
 
     dma("S", T.hl[:, 0:V0], T.h0[:, I:I + V0], [], [X("hl", 0, V0)])
@@ -204,90 +210,90 @@ def rank_program(g, core, T, topo):
     dma("S", T.hi[:, :], T.h0[:, 0:I], [], [X("hi", 0, 1024)])
 
     vset(X("ones", 0, 128), 1.0)
-    giota(X("nf", 0, 64), [[0, 8], [1, 8]], -2048, 8)
+    giota(X("nrow", 0, 512), [[1, 512]], 1024, 0)
+    act(X("PA", D, D + 128), X("ones", 0, 128), AF.Silu, scale=0.0)
+    vset(X("PW", D, OWN), 0.0)
+    act(X("nrow", 512, 1024), X("nrow", 0, 512), bias=512.0)
+    act(X("PA", D + 128, D + 640), X("nrow", 0, 512), scale=0.0)
+    act(X("PA", D + 640, OWN), X("nrow", 0, 384), scale=0.0)
     gsel(ID, X("ones", 0, 128), [[-1, 128]], OP.is_equal, 0, 1)
-    emit("V", [lambda: g.vector.memset(T.XC[:], 0.0)], [], [(None, "XC", 0, 16)])
-    vcopy(part("XC", 0), X("nf", 0, 64))
-    vtt(part("XC", 1), X("nf", 0, 64), part("XC", 0), OP.subtract)
-    for h in range(2):
-        spread("XC", h)
-    vset(X("PW", 0, 1040), 0.0)
-    for r in range(RO):
-        vset(X("H%d" % r, I, OWN), 0.0)
+    giota(X("nf", 0, 64), [[0, 8], [1, 8]], 1024, 8)
+    giota(X("BS", 0, 16), [[-2, 2], [0, 8]], 1, 0)
+    giota(X("H0", 0, D), [[0, D]], 0, 0)
+    gsel(X("BS", 0, 16), X("BS", 0, 16), [[0, 2], [-16, 8]], OP.is_ge, 0, 1)
+    gsel(X("O32", 0, 8), X("ones", 0, 8), [[-16, 8]], OP.is_equal, 0, 1)
+    gsel(X("BS", 0, 16), X("BS", 0, 16), [[0, 2], [16, 8]], OP.is_ge, 15, -1)
     vset(X("KW", 0, 272), 0.0)
     emit("V", [lambda: g.vector.memset(T.L[:, 0:193:2, :], 0.0)], [], [(None, "L", 0, 1544)])
-    gsel(X("WP", 0, 32), X("ones", 0, 32), [[-2, 4], [-16, 8]], OP.is_ge, 0, 1)
-    gsel(X("WP", 0, 32), X("WP", 0, 32), [[2, 4], [16, 8]], OP.is_ge, 1, -1)
-    gsel(X("BS", 0, 8), X("ones", 0, 8), [[-16, 8]], OP.is_ge, 0, 1)
-    gsel(X("BS", 0, 8), X("BS", 0, 8), [[16, 8]], OP.is_ge, 15, -1)
-    for nm in ("H0", "H1", "H2", "hcl", "hcr", "GW", "CW"):
-        giota(X(nm, 0, D), [[0, D]], 0, 0)
-    act(X("nrow", 0, 512), X("b0", 0, 512))
-    act(X("nrow", 512, 1024), X("b1", 0, 512))
-    vts(X("su", 0, 42), X("si", 0, 42), float(D), OP.add)
-    vcopy(X("H0", OWN, GHO), X("hl", 0, V0))
-    act(X("s0", 0, 320), ind(X("H0", I, GHO), X("su", 0, 20)))
-    vcopy(X("s0", 320, 672), ind(X("H0", I, GHO), X("su", 20, 42)))
+    vcopy(X("su", 0, 42), X("si", 0, 42))
+    for call in sends(T, topo, rank, True):
+        for d in sorted(call):
+            if d - 1 not in call:
+                e = min(x for x in range(d, 9) if x not in call)
+                vcopy(X("s0", GH * (d - 1), GH * (e - 1)), ind(X("hl", 0, V0), X("su", 6 * (d - 1), 6 * (e - 1))))
     vts(X("KU", 0, 128), X("KI", 0, 128), float(D), OP.add)
 
-    mine = sends(T, topo, rank)
-    narr = sum(len(sends(T, topo, (rank - d) % 8)[d]) for d in range(1, 8))
     nsent = [0]
     for r in range(RO):
+        narr = sum(len(call[d]) for d in range(1, 8) for call in sends(T, topo, (rank - d) % 8, r == 0) if d in call)
         cnt["arr%d" % r] = narr
         acc.setdefault("H%d" % r, []).append((True, GHO, WIN, ("arr%d" % r, narr, "R", {})))
 
     def exchange(r):
-        sync("G", hazards("G", [X("s%d" % r, 0, 672)], []))
-        tr = []
-        for d in range(1, 8):
-            rid, pid, _ = topo.addr(T.cores[(rank + d) % 8])
-            tr.append(RemoteDMATransfer(src=T["s%d" % r][:, GH * (d - 1):GH * d], dst=T["H%d" % r][:, GHO + GH * (d - 1):GHO + GH * d],
-                                        dst_ids=[DstId(rid=rid, pnc=pid)], dma_engine_mask=sum(1 << e for e in mine[d]),
-                                        remote_sem=T.sem["arr%d" % r]))
-            nsent[0] += len(mine[d])
-        g.remote_dma_fused(tr, local_sem=T.sem.sent)
+        for call in sends(T, topo, rank, r == 0):
+            sync("G", hazards("G", [X("s%d" % r, GH * (d - 1), GH * d) for d in call], []))
+            tr = []
+            for d, engines in call.items():
+                rid, pid, _ = topo.addr(T.cores[(rank + d) % 8])
+                tr.append(RemoteDMATransfer(src=T["s%d" % r][:, GH * (d - 1):GH * d],
+                                            dst=T["H%d" % r][:, GHO + GH * (d - 1):GHO + GH * d], dst_ids=[DstId(rid=rid, pnc=pid)],
+                                            dma_engine_mask=sum(1 << e for e in engines), remote_sem=T.sem["arr%d" % r]))
+                nsent[0] += len(engines)
+            g.remote_dma_fused(tr, local_sem=T.sem.sent)
     exchange(0)
-    gsel(X("vo", 0, V0), X("vi", 0, V0), [[0, V0]], OP.is_ge, 0, 0)
-    gsel(X("H0", D, OWN), X("hi", 0, I), [[0, I]], OP.is_ge, 0, 0)
 
-    def scatter(a):
-        vcopy(ind(X("PW", 0, WIN), X("KU", a, a + 64)), X("nrow", 0, 1024))
-
-    scatter(0)
+    emit("A", [lambda: g.scalar.activation(T.PA[:, 0:WIN].indirect(T.KU[:, 64:128]), T.nrow[:, :], AF.Silu)],
+         [X("nrow", 0, 1024), X("KU", 64, 128)], [X("PA", 0, WIN)])
+    vcopy(X("H0", OWN, GHO), X("hl", 0, V0))
+    vcopy(X("vo", 0, V0), X("vi", 0, V0))
+    vcopy(ind(X("PW", 0, WIN), X("KU", 0, 64)), X("nrow", 0, 1024))
+    vset(X("H1", I, OWN), 0.0)
+    vts(X("su", 0, 42), X("si", 0, 42), float(D), OP.add)
     for s in range(2):
         vcopy(X("KW", 136 * s + 1, 136 * s + 129, 2), X("KI", 64 * s, 64 * s + 64))
+    vcopy(X("H0", D, OWN), X("hi", 0, I))
     for j in range(2):
-        vts(X("nid", 64 * j, 64 * j + 64), X("nf", 0, 64), 2048.0, OP.add)
-    scatter(64)
-    for nm, w in (("idn", -1.0), ("idh", 0.5), ("idhn", -0.5), ("idq", -0.25), ("ide", 2.0 ** -13), ("idf", -2.0 ** -13),
-                  ("idk", -2048.0)):
-        act(X(nm, 0, 128), ID, scale=w)
-    act((T.XG[:], "XG", 0, 16), X("nrow", 0, 1024), scale=0.0)
+        vts(X("nid", 64 * j, 64 * j + 64), X("nf", 0, 64), -1024.0, OP.add)
+    vts(X("KC", 0, 128), X("KU", 0, 128), float(OWN), OP.min)
     for nm in ("hcl", "hcr"):
-        act(X(nm, OWN, OWN + 1024), X("nrow", 0, 1024), scale=0.0, bias=255.0)
-        act(X(nm, WIN - 1, WIN), X("nrow", 0, 1), scale=0.0, bias=255.0)
+        vset(X(nm, 0, D), 0.0)
+        vset(X(nm, OWN, OWN + 1), 255.0)
+    giota(X("CQ", 0, 256), [[0, 64], [1, 4]], 0, 0)
+    gsel(X("msk", 0, 256), X("CQ", 0, 256), [[0, 64], [-1, 4]], OP.is_ge, 0, 0, 1.0)
+    giota((T.XG[:, :, 8:16, :], "XG", 8, 16), [[0, 512]], 0, 0)
+    diagonal(("idq", -0.25))
+    for nm in ("GW", "CW"):
+        giota(X(nm, OWN, OWN + 1), [[0, 1]], 0, 0)
+    for nm in ("GW", "CW", "H1", "H2"):
+        giota(X(nm, 0, D), [[0, D]], 0, 0)
+    giota(X("H2", I, OWN), [[0, D]], 0, 0)
+
+    def moved(r):
+        plus("b1", [(0, V0, "id1", X("H%d" % r, OWN, GHO)), (0, V0, "id1", X("vo", 0, V0))], True)
 
     def leaves(r):
-        plus("b2", [(0, V0, "id1", X("H%d" % r, OWN, GHO)), (0, V0, "id1", X("vo", 0, V0))], True)
-        act(X("y1", 0, V0), X("b2", 0, V0), AF.Relu, scale=-1.0, bias=255.0)
+        act(X("y1", 0, V0), X("b1", 0, V0), AF.Relu, scale=-1.0, bias=255.0)
         act(X("OH", I, I + V0) if r == RO - 1 else X("H%d" % (r + 1), OWN, GHO), X("y1", 0, V0), AF.Relu, scale=-1.0, bias=255.0)
 
     def ghosts(r):
         act(X("s%d" % r, 0, 672), ind(X("H%d" % r, I, GHO), X("su", 0, 42)))
-        exchange(r)
 
+    moved(0)
     leaves(0)
-    giota(X("CQ", 0, 256), [[0, 64], [1, 4]], 0, 0)
+    gsel(X("WP", 0, 32), X("ones", 0, 32), [[-2, 4], [-16, 8]], OP.is_ge, 0, 1)
+    gsel(X("OC", 0, 8), X("ones", 0, 8), [[-16, 8]], OP.is_equal, -10, 1)
+    gsel(X("WP", 0, 32), X("WP", 0, 32), [[2, 4], [16, 8]], OP.is_ge, 1, -1)
     ghosts(1)
-    giota(X("GW", OWN, WIN), [[0, WIN - OWN]], 0, 0)
-    giota(X("CE", 0, 256), [[1, 4], [0, 64]], -4, 0)
-    gsel(X("WG", 16, 48), X("ones", 0, 32), [[0, 4], [-16, 8]], OP.is_ge, -2, 1)
-    gsel(X("WG", 16, 48), X("WG", 16, 48), [[0, 4], [16, 8]], OP.is_ge, 5, -1)
-    giota(X("WC", 0, 32), [[0, 4], [-32, 8]], -1, 2)
-    gsel(X("WC", 0, 32), X("WC", 0, 32), [[0, 4], [-16, 8]], OP.is_ge, 0, 1)
-    gsel(X("WC", 0, 32), X("WC", 0, 32), [[0, 4], [16, 8]], OP.is_ge, 1, -1)
-    gsel(X("OC", 0, 8), X("ones", 0, 8), [[-16, 8]], OP.is_equal, -2, 1)
 
     NID = X("nid", 0, 64)
     ONE = X("ones", 0, 64)
@@ -302,162 +308,184 @@ def rank_program(g, core, T, topo):
               for s in range(2) for h in range(2)], [X("KW", 0, 272), ID], True)
     rounded(2, "b5", 0)
     rounded(4, "b5", 64)
-    act(X("BS", 8, 16), X("BS", 0, 8), scale=-1.0)
-    act(X("msk", 0, 256), X("CQ", 0, 256), AF.Sign)
-    act(X("WG", 0, 8), X("WP", 0, 8))
-    act(X("WG", 8, 16), X("WP", 16, 24))
-    act(X("WG", 48, 56), X("WP", 24, 32))
-    act(X("WR", 0, 8), X("WP", 0, 8), scale=-2.0 ** -13)
-    act(X("WR", 8, 24), X("WP", 8, 24))
-    act(X("sPP", 0, 144), X("nrow", 0, 144), scale=0.0)
-    act(X("sPP", 16, 144, 16), X("WP", 24, 32))
-    wrap("b6", 64, "PW", D, X("WP", 0, 8), True)
+    wrap("b6", 64, "PA", D, X("O32", 0, 8))
+    wrap("b6", 64, "PW", D, X("O32", 0, 8), True)
+
+    def gcopy(out, in_):
+        gsel(out, in_, [[0, in_[3] - in_[2]]], OP.is_ge, 0, 0)
 
     BSP, BSN = X("BS", 0, 8), X("BS", 8, 16)
     GA = X("gq", 3, 256, 4)
-    NA = 8 * QA
+    ROT, CHOICE, SIDE = part("XG", 8), X("cd", 0, 64), part("XG", 10)
+    NA = 512
     for r in range(RO):
         last = r == RO - 1
         win = X("H%d" % r, 0, WIN)
-        wl, wr = X("hcl", 0, WIN), X("hcr", 0, WIN)
-
-        def gain(row, off, w, ch, end=False, nq=128):
-            wrap("b4", ch, row, off, w, end, 32, 4, nq)
+        wl, wr = X("hcl", 0, OWN + 1), X("hcr", 0, OWN + 1)
 
         act(X("hcl", D, OWN), ind(win, X("KU", 0, 64)))
         vcopy(X("hcr", D, OWN), ind(win, X("KU", 64, 128)))
         if r:
             vts(X("E2", 0, 192), X("b3", 0, 192), 0.0, OP.is_equal)
+            rest(2, "b5", 0)
             vtt(lists(W0, 3), X("b7", 256, 448), X("E2", 0, 192), OP.mult)
-        gsel(X("hr2", NA, 1024), X("hcr", D + NA, OWN), [[0, 1024 - NA]], OP.is_ge, 0, 0)
+        else:
+            vts(X("idn", 0, 128), ID, -1.0, OP.mult)
+            vcopy(part("XG", 6), X("b6", 64, 128))
+        (gcopy if r else vcopy)(X("hr2", NA, 1024), X("hcr", D + NA, OWN))
         if not r:
-            giota(X("CW", OWN, WIN), [[0, WIN - OWN]], 0, 0)
-        plus("b4", [(0, 256, "idq", X("CQ", 0, 256))])
-        act(X("zz", 0, 512), ind(wl, X("KU", 64, 96)))
-        act(X("zz", 512, 1024), ind(wl, X("KU", 96, 128)))
-        act(X("zz", 1024, 1024 + NA), ind(wr, X("KU", 0, NA // 16)))
-        vtt(X("mm", 1024, 2048), ind(wl, X("KU", 0, 64)), X("hcr", D, OWN), OP.max)
-        vtt(X("mm", 2048, 3072), ind(wr, X("KU", 64, 128)), X("hcl", D, OWN), OP.max)
-        vtt(X("mm", NA, 1024), ind(wr, X("KU", NA // 16, 64)), X("hr2", NA, 1024), OP.max)
-        gain("hcl", D, BSP, 0)
-        gain("hcl", D, BSP, 1)
-        plus("b0", [(0, 512, "idn", X("hcl", D, D + 512)), (0, 512, "id1", X("zz", 0, 512))], True)
-        gain("hcl", D, BSN, 3)
+            giota(X("sPP", 0, 144), [[0, 144]], 0, 0)
+            gsel(X("WG", 16, 48), X("ones", 0, 32), [[0, 4], [-16, 8]], OP.is_ge, -2, 1)
+            diagonal(("idk", 1024.0), ("ide", 2.0 ** -13), ("idf", -2.0 ** -13))
+            gcopy(X("WG", 0, 8), X("WP", 0, 8))
+            gcopy(X("WG", 8, 16), X("WP", 16, 24))
+            gcopy(X("WG", 48, 56), X("WP", 24, 32))
+            gsel(X("WG", 16, 48), X("WG", 16, 48), [[0, 4], [16, 8]], OP.is_ge, 5, -1)
+            gcopy(X("WR", 8, 24), X("WP", 8, 24))
+            gsel(X("sPP", 16, 144, 16), X("WP", 24, 32), [[0, 8]], OP.is_ge, 0, 0)
+            exchange(1)
+            diagonal(("idh", 0.5), ("idhn", -0.5))
+            giota(X("WC", 0, 32), [[0, 4], [-32, 8]], -17, 2)
+            gsel(X("WC", 0, 32), X("WC", 0, 32), [[0, 4], [-16, 8]], OP.is_ge, -8, 1)
+            giota(X("CE", 0, 256), [[1, 4], [0, 64]], -4, 0)
+            gsel(X("WC", 0, 32), X("WC", 0, 32), [[0, 4], [16, 8]], OP.is_ge, 9, -1)
+        if not last:
+            moved(r + 1)
+        act(X("zz", 0, 512), ind(wl, X("KC", 64, 96)))
+        act(X("zz", 512, 1024), ind(wl, X("KC", 96, 128)))
+        act(X("zz", 1024, 1024 + NA), ind(wr, X("KC", 0, NA // 16)))
+        vtt(X("mm", 1024, 2048), ind(wl, X("KC", 0, 64)), X("hcr", D, OWN), OP.max)
+        vtt(X("mm", 2048, 3072), ind(wr, X("KC", 64, 128)), X("hcl", D, OWN), OP.max)
+        vtt(X("mm", NA, 1024), ind(wr, X("KC", NA // 16, 64)), X("hr2", NA, 1024), OP.max)
         if r:
-            plus("b6", [(64, 64, "id1", lists(a)) for a in (PAR, W0, W1, XX)])
-            aslist("b6", 0, (PAR, W0, W1, XX), True)
-        plus("b3", [(0, 512, "idn", X("hcl", D + 512, OWN)), (0, 512, "id1", X("zz", 512, 1024))], True)
+            plus("b4", [(0, 256, "idq", X("CQ", 0, 256))])
         gain("hcr", D, BSP, 2)
         gain("hcr", D, BSP, 3)
-        gain("hcr", D, BSN, 0, False, QA)
+        gain("hcl", D, BSP, 0)
+        plus("b0", [(0, 512, "idn", X("hcl", D, D + 512)), (0, 512, "id1", X("zz", 0, 512))], True)
+        if r:
+            plus("b6", [(64, 64, "id1", lists(a)) for a in (PAR, W0, W1, XX)], True)
+        gain("hcl", D, BSP, 1)
+        plus("b3", [(0, 512, "idn", X("hcl", D + 512, OWN)), (0, 512, "id1", X("zz", 512, 1024))], True)
+        gain("hcl", D, BSN, 3)
+        gain("hcr", D, BSN, 0, False, NA // 8)
+        if not r:
+            plus("b4", [(0, 256, "idq", X("CQ", 0, 256))])
         plus("b2", [(0, NA, "idn", X("hcr", D, D + NA)), (0, NA, "id1", X("zz", 1024, 1024 + NA))], True)
-        if not last:
-            rounded(6, "b6", 64)
         act(X("mm", 3072, 3584), X("b0", 0, 512), AF.Relu)
+        if r == 1:
+            rounded(6, "b6", 64)
         gain("mm", 1024, BSN, 1)
         act(X("mm", 3584, 4096), X("b3", 0, 512), AF.Relu)
         act(X("mm", 0, NA), X("b2", 0, NA), AF.Relu)
         gain("mm", 2048, BSN, 2)
         gain("mm", 3072, BSN, 3)
         gain("mm", 0, BSN, 0, True)
-        if r < 2:
+        if not last:
             leaves(r + 1)
+        if not r:
+            act(X("WC", 32, 40), X("OC", 0, 8), scale=-0.5)
+            act(X("WR", 0, 8), X("WP", 0, 8), scale=-2.0 ** -13)
         if r == 1:
             dma("S", T.yh[:, I:I + V0], T.OH[:, I:I + V0], [X("OH", I, I + V0)], [])
-        rest(2, "b5", 0)
+        vcopy(lists(PAR), X("b6", 64, 128))
+        if not r:
+            rest(2, "b5", 0)
         rest(4, "b5", 64)
         vcopy(lists(KL, 2), X("b5", 0, 128))
-        if not last:
+        if r == 1:
             rest(6, "b6", 64)
-            vcopy(lists(PAR), X("b6", 64, 128))
+        elif not r:
+            vtt(part("XG", 7), lists(PAR), part("XG", 6), OP.subtract)
         emit("V", [lambda: g.vector.tensor_tensor_scan(T.gq[:, :], T.msk[:, :], T.b4[:, 0:256], 0.0, OP.mult, OP.max)],
              [X("msk", 0, 256), X("b4", 0, 256)], [X("gq", 0, 256)])
+        vtt(X("TB", 128, 192), X("b6", 64, 128), X("nf", 0, 64), OP.is_gt)
+        aslist("b6", 0, (PAR,), True)
         vcopy(part("XG", 0), GA)
+        vts(X("gi", 0, 64), GA, 0.375, OP.add)
         vtt(part("XG", 1), GA, part("XG", 0), OP.subtract)
-        if not r:
-            aslist("b6", 0, (PAR,), True)
         spread("XG", 0)
         spread("XG", 1)
-        vtt(X("TB", 128, 192), X("b6", 64, 128), X("nf", 0, 64), OP.is_gt)
-        vts(X("PB", 0, 64), X("b6", 0, 64), 2048.0 + D, OP.add)
+        vts(X("PB", 0, 64), X("b6", 0, 64), D - 1024.0, OP.add, 0.0, OP.max)
         vtt(X("TB", 0, 128), X("b5", 0, 128), X("nid", 0, 128), OP.is_gt)
-        vts(X("gi", 0, 64), GA, 0.375, OP.add)
-        vtt(part("XC", 1), X("gi", 0, 64), GA, OP.subtract)
+        vtt(CHOICE, X("gi", 0, 64), GA, OP.subtract)
         act(X("GW", D, D + 512), X("b0", 0, 512))
         vcopy(X("GW", D + 512, OWN), X("b1", 0, 512))
-        gwin = X("GW", 0, WIN)
+        gwin = X("GW", 0, OWN + 1)
         plus("b7", [(0, 64, "id1", X("TB", 128, 192)), (128, 128, "idn", lists(KL, 2)), (64, 64, "idn", NID),
                     (128, 128, "idn", X("nid", 0, 128))])
         if not last:
             plus("b7", [(256, 128, "idk", X("ones", 0, 128)), (256, 128, "idn", X("nid", 0, 128))]
                  + [(oc, 64, "idn", lists(PAR)) for oc in (256, 320, 384)])
         plus("b5", [(0, 64, "id1", X("TB", 0, 64)), (64, 64, "idn", lists(KR)), (128, 64, "idn", lists(KR))])
-        plus("b6", [(0, 64, "ide", part("XG", 0)), (0, 64, "ide", part("XG", 1)), (0, 64, "ide", part("XC", 1)),
+        plus("b6", [(0, 64, "ide", part("XG", 0)), (0, 64, "ide", part("XG", 1)), (0, 64, "ide", CHOICE),
                     (0, 64, "idf", X("TB", 64, 128)), (64, 64, "idn", lists(KL)), (128, 64, "idn", lists(KL))])
-        if not r:
-            act(X("WC", 32, 40), X("OC", 0, 8), scale=-0.5)
 
         def both(buf, w, lst, o, cut):
             act(X(buf, 0, cut), ind(w, X(lst, o, o + cut // 16)))
             vcopy(X(buf, cut, 1024), ind(w, X(lst, o + cut // 16, o + 64)))
 
         both("gp", gwin, "PB", 0, 512)
-        both("gl", gwin, "KU", 0, 512)
-        both("gr", gwin, "KU", 64, 512)
+        both("gl", gwin, "KC", 0, 512)
+        both("gr", gwin, "KC", 64, 512)
         wrap("b7", 0, "gp", 0, X("WG", 0, 32 if last else 56), True)
         if not last:
             pe("b4", [(T.b4[:, 256:320], T.sPP[:, 16 - k:144 - k], T.gp[:, k:1024:16]) for k in range(16)],
                [X("sPP", 0, 144), X("gp", 0, 1024)], True)
         wrap("b5", 0, "gl", 0, X("WP", 0, 24), True)
         wrap("b6", 0, "gr", 0, X("WR", 0, 24), True)
+        act(part("XG", 9), CHOICE)
         if not r:
             ghosts(2)
+            exchange(2)
         vts(X("ee", 0, 64), X("b7", 0, 64), 1.0, OP.max)
-        vts(part("XC", 2), X("b7", 64, 128), 0.0, OP.is_equal)
+        vts(SIDE, X("b7", 64, 128), 0.0, OP.is_equal)
         vtt(X("ee", 64, 128), X("b5", 0, 64), X("ee", 0, 64), OP.max)
         if not last:
-            vts(X("PPu", 0, 64), X("b4", 256, 320), 2048.0 + D, OP.add)
+            vts(X("PPu", 0, 64), X("b4", 256, 320), D - 1024.0, OP.add, 0.0, OP.max)
         vtt(X("ee", 128, 192), X("ee", 64, 128), X("gi", 0, 64), OP.is_gt)
-        vtt(part("XC", 0), X("b6", 0, 64), X("ee", 128, 192), OP.is_ge)
-        spread("XC", 0)
-        spread("XC", 1)
-        vtt(X("cod", 0, 64), part("XC", 1), part("XC", 0), OP.subtract)
+        vtt(ROT, X("b6", 0, 64), X("ee", 128, 192), OP.is_ge)
+        spread("XG", 0)
+        spread("XG", 1)
+        vtt(X("cod", 0, 64), CHOICE, ROT, OP.subtract)
         for j in range(4):
             vts(X("MK", 64 * j, 64 * j + 64), X("cod", 0, 64), 0.25 * j - 1.0, OP.is_equal)
         act(X("CW", D, D + 512), X("b0", 0, 512))
         vcopy(X("CW", D + 512, OWN), X("b1", 0, 512))
-        cwin = X("CW", 0, WIN)
-        SIDE = part("XC", 2)
+        cwin = X("CW", 0, OWN + 1)
         plus("b2", [(0, 128, "idq", X("CE", 0, 128)), (0, 64, "idhn", SIDE), (64, 64, "idhn", SIDE)])
         both("cp", cwin, "PB", 0, 512)
-        aslist("b4", 0, (KL,))
-        aslist("b4", 64, (KR,))
+        aslist("b4", 0, (KR,))
         if not last:
             plus("b3", [(0, 128, "idq", X("CE", 128, 256)), (128, 64, "id1", ONE), (0, 64, "idh", SIDE), (64, 64, "idh", SIDE),
                         (128, 64, "idq", SIDE)])
         wrap("b2", 0, "cp", 0, X("WC", 0, 16), True)
         vtt(lists(P0, 2), X("b5", 64, 192), X("MK", 0, 128), OP.mult)
         vtt(lists(P2, 2), X("b6", 64, 192), X("MK", 128, 256), OP.mult)
-        aslist("b4", 64, (P0, P1))
-        aslist("b4", 0, (P2, P3))
+        aslist("b4", 0, (P0, P1))
+        aslist("b1", 0, (KL, P2, P3))
         if not last:
             act(X("cg", 0, CG), ind(cwin, X("PPu", 0, CG // 16)))
-        vts(X("E1", 0, 128), X("b2", 0, 128), 0.0, OP.is_equal)
-        vtt(lists(TL, 2), X("b7", 128, 256), X("E1", 0, 128), OP.mult)
-        aslist("b4", 0, (TL,))
-        aslist("b4", 64, (TR,), True)
+        vts(X("E1", 64, 128), X("b2", 64, 128), 0.0, OP.is_equal)
+        vts(X("E1", 0, 64), X("b2", 0, 64), 0.0, OP.is_equal)
+        vtt(lists(TR), X("b7", 192, 256), X("E1", 64, 128), OP.mult)
+        vtt(lists(TL), X("b7", 128, 192), X("E1", 0, 64), OP.mult)
+        aslist("b4", 0, (TR,), True)
+        aslist("b1", 0, (TL,), True)
         plus("b5", [(0, 128, "id1", lists(KL, 2)), (0, 64, "id1", lists(P2)), (0, 64, "id1", lists(P3)),
                     (64, 64, "id1", lists(P0)), (64, 64, "id1", lists(P1)), (0, 128, "id1", lists(TL, 2))], True)
-        vts(X("KU", 0, 128), X("b4", 0, 128), float(D), OP.add)
+        vts(X("KU", 64, 128), X("b4", 0, 64), float(D), OP.add)
+        vts(X("KU", 0, 64), X("b1", 0, 64), float(D), OP.add)
         cuts = (0, 128, 448, 768, 1024) if last else CUTS
-        if last:
+        for j, (a, b) in enumerate(zip(cuts, cuts[1:])):
+            (act if j else vcopy)(X("rr", a, b), ind(win, X("KU", 64 + a // 16, 64 + b // 16)))
+        if not last:
+            vts(X("KC", 0, 128), X("KU", 0, 128), float(OWN), OP.min)
+        else:
             vcopy(lists(KL, 2), X("b5", 0, 128))
             for h in range(2):
                 pe("b0", [(T.b0[64 * h:64 * h + 64, b:512:8], T.L[:, 1:129:2, b], T.id1[:, 8 * h:8 * h + 8, :]) for b in range(8)],
                    [lists(KL, 8), ID], True)
-        for j, (a, b) in enumerate(zip(cuts, cuts[1:])):
-            (act if j else vcopy)(X("rr", a, b), ind(win, X("KU", 64 + a // 16, 64 + b // 16)))
-        if last:
             act(X("OK", 0, 512), X("b0", 0, 512))
             for h in range(2):
                 for s in range(2):

from concourse.bass import DstId, RemoteDMATransfer
from concourse.mybir import AluOpType, ActivationFunctionType

OP = AluOpType
AF = ActivationFunctionType
I, V0, GH, RO = 1024, 353, 96, 3
D = 7
OWN, GHO, WIN = I + D, I + V0 + D, 2049 + D
KL, KR, P2, P3, P0, P1, TL, TR, PAR, W0, W1, XX = range(12)
CG = 704
CUTS = (0, 192, 608, 1024)

SCRATCH = {"b%d" % _b: ("psum", [128, 512], "float32") for _b in range(8)}
for _dt, _names in (
        ("int32", "hl 360 hi 1024 vi 360 si 48 KI 128 gi 64"),
        ("uint16", "su 48 KU 128 KC 128 PB 64 PPu 64"),
        ("float16", "KW 272 nid 128"),
        ("bfloat16", "H0 2064 H1 2064 H2 2064 vo 368 s0 672 s1 672 s2 672 hcl 1040 hcr 1040 hr2 1024 mm 4096 zz 2048 rr 1024 "
                     "GW 1040 CW 1040 gl 1024 gr 1024 gp 1024 cp 1024 cg 1024 ones 128 idn 128 idh 128 idhn 128 "
                     "idq 128 ide 128 idf 128 idk 128 WP 32 WG 56 WR 24 OC 24 WC 40 BS 64 sPP 144 CQ 256 CE 320 msk 256 TB 192 "
                     "cd 64 cod 64 MK 256 E1 128 E2 192"),
        ("float32", "nf 64 gq 256 ee 192 y1 360 OK 512 OH 1384 PW 2064 PA 2064 nrow 1024 O32 8")):
    _w = _names.split()
    for _n, _c in zip(_w[::2], _w[1::2]):
        SCRATCH[_n] = ("sbuf", [128, int(_c)], _dt)
SCRATCH["L"] = ("sbuf", [128, 193, 8], "float16")
SCRATCH["id1"] = ("sbuf", [128, 16, 8], "bfloat16")
SCRATCH["XG"] = ("sbuf", [128, 8, 16, 8], "bfloat16")
SEMAPHORES = ["V", "A", "P", "G", "arr0", "arr1", "arr2", "sent"] + ["d%d" % _i for _i in range(20)]


def sends(T, topo, q, urgent):
    src = T.cores[q]
    dst = {d: T.cores[(q + d) % 8] for d in range(1, 8)}
    near = [d for d in dst if topo.chip(dst[d]) == topo.chip(src)]
    far = [d for d in dst if d not in near]
    pool = list(topo.engines(src, dst[far[0]]))

    def direct(d):
        a, b = topo.chip(src), topo.chip(dst[d])
        return topo.mates(a, b) or topo.same_plane(a, b)
    far.sort(key=lambda d: (direct(d), d))
    n = 1 << len(far).bit_length() - 1
    rest = [e for e in topo.engines(src, dst[near[0]]) if e not in pool][:len(pool) // n]
    if not urgent:
        spare = len(pool) - len(far)
        call = {d: pool[2 * j:2 * j + 2] if j < spare else pool[spare + j:spare + j + 1] for j, d in enumerate(far)}
        call[near[0]] = rest
        return [call]
    calls = []
    for ds in (far[:n], far[n:]):
        k = len(pool) // len(ds)
        calls.append({d: pool[k * j:k * j + k] for j, d in enumerate(ds)})
    calls[1][near[0]] = rest
    return calls


def rank_program(g, core, T, topo):
    rank = T.rank_of(core)
    if rank is None:
        return
    queue = {"V": g.vector, "A": g.scalar, "P": g.tensor, "G": g, "S": g.sync}
    cnt = {}
    known = {q: {} for q in queue}
    acc = {}
    ndma = [0]

    def psum(name):
        return name[0] == "b" and name[1:].isdigit()

    def hazards(q, rd, wr):
        deps = []
        for ops, w in ((rd, False), (wr, True)):
            for _, name, a, b in ops:
                if psum(name):
                    deps += [r for qq, r in acc.setdefault(name, {}).items() if qq != q]
                    continue
                for k, x, y, r in acc.setdefault(name, []):
                    if x < b and y > a and (w or k) and not (r[2] == q and (q == "P" or not k)):
                        deps.append(r)
        return deps

    def note(q, rd, wr, rec):
        for ops, w in ((rd, False), (wr, True)):
            for _, name, a, b in ops:
                if psum(name):
                    acc[name][q] = rec
                    continue
                lst = acc[name]
                if w:
                    lst[:] = [t for t in lst if not (t[1] >= a and t[2] <= b)]
                else:
                    lst[:] = [t for t in lst if t[0] or t[3][2] != rec[2] or not (t[1] >= a and t[2] <= b)]
                lst.append((w, a, b, rec))

    def sync(q, deps):
        kn = known[q]
        best = {}
        for r in deps:
            if kn.get(r[0], 0) < r[1] and (r[0] not in best or best[r[0]][1] < r[1]):
                best[r[0]] = r
        for r in sorted(best.values(), key=lambda r: -len(r[3])):
            if kn.get(r[0], 0) >= r[1]:
                continue
            queue[q].wait_ge(T.sem[r[0]], r[1])
            for s, c in r[3].items():
                kn[s] = max(kn.get(s, 0), c)
            kn[r[0]] = r[1]

    def emit(q, fns, rd, wr):
        sync(q, hazards(q, rd, wr))
        for f in fns:
            f().then_inc(T.sem[q], 1)
            cnt[q] = cnt.get(q, 0) + 1
        note(q, rd, wr, (q, cnt[q], q, dict(known[q])))

    def dma(q, out, in_, rd, wr):
        sync(q, hazards(q, rd, wr))
        s = "d%d" % ndma[0]
        ndma[0] += 1
        cnt[s] = 16
        queue[q].dma_start(out, in_).then_inc(T.sem[s], 16)
        note("D", rd, wr, (s, 16, "D", dict(known[q])))

    def X(name, a, b, step=1):
        return (T[name][:, a:b] if step == 1 else T[name][:, a:b:step], name, a, b)

    def part(name, p):
        return (T[name][:, :, p, :], name, p, p + 1)

    def lists(a, n=1):
        return (T.L[:, 16 * a + 1:16 * (a + n):2, :], "L", 128 * a + 8, 128 * (a + n))

    def ind(win, off):
        return (win[0].indirect(off[0]), win, off)

    def flat(*ops):
        out = []
        for o in ops:
            out += [o[1], o[2]] if len(o) == 3 else [o]
        return out

    def vcopy(out, in_):
        if len(out) == 3:
            emit("V", [lambda: g.vector.tensor_copy(out[0], in_[0])], [in_, out[2]], [out[1]])
        else:
            emit("V", [lambda: g.vector.tensor_copy(out[0], in_[0])], flat(in_), [out])

    def vtt(out, a, b, op):
        emit("V", [lambda: g.vector.tensor_tensor(out[0], a[0], b[0], op)], flat(a, b), [out])

    def vts(out, a, s1, op0, s2=None, *op1):
        emit("V", [lambda: g.vector.tensor_scalar(out[0], a[0], s1, s2, op0, *op1)], [a], [out])

    def vset(out, c):
        emit("V", [lambda: g.vector.memset(out[0], c)], [], [out])

    def act(out, in_, func=AF.Copy, **kw):
        emit("A", [lambda: g.scalar.activation(out[0], in_[0], func, **kw)], flat(in_), [out])

    def gsel(out, in_, pattern, op, base, cm, fill=0.0):
        emit("G", [lambda: g.affine_select(out[0], in_[0], pattern, op, fill, base, cm)], [in_], [out])

    def giota(out, pattern, base, cm):
        emit("G", [lambda: g.iota(out[0], pattern, base, cm, allow_small_or_imprecise_dtypes=True)], [], [out])

    def diagonal(*names):
        for nm, w in names:
            gsel(X(nm, 0, 128), (T.XG[:, 0:4, 12:16, :], "XG", 12, 16), [[-1, 128]], OP.not_equal, 0, 1, w)

    ID = (T.id1[:, :, :], "id1", 0, 128)
    opened = set()

    def pe(bank, terms, rd, last):
        fns = []
        for j, (o, l, r) in enumerate(terms):
            first = bank not in opened
            opened.add(bank)
            fns.append(lambda o=o, l=l, r=r, a=first, z=last and j == len(terms) - 1: g.tensor.matmul(o, l, r, a, z))
        if last:
            opened.discard(bank)
        emit("P", fns, rd, [X(bank, 0, 512)])

    def plus(bank, terms, last=False):
        dg = [ID if t[2] == "id1" else X(t[2], 0, 128) for t in terms]
        pe(bank, [(X(bank, t[0], t[0] + t[1])[0], d[0], t[3][0]) for t, d in zip(terms, dg)], dg + [t[3] for t in terms], last)

    def wrap(bank, oc, row, off, w, last=False):
        n = w[3] - w[2]
        pe(bank, [(T[bank][:, oc + b:oc + 8 * n:8], T[row][:, off + b:off + 1024:8], w[0]) for b in range(8)],
           [X(row, off, off + 1024), w], last)

    def gain(row, off, w, ch, last=False, nq=128):
        pe("b4", [(T.b4[0:nq, 4 * b + ch:256:32], T[row][:, off + b:off + 8 * nq:8], w[0]) for b in range(8)],
           [X(row, off, off + 1024), w], last)

    def spread(buf, h):
        pe("b%d" % h, [(T["b%d" % h][:, b:512:8], T[buf][:, :, :, b], T.id1[:, 8 * h:8 * h + 8, :]) for b in range(8)],
           [(None, buf, 0, 16), ID], True)

    def aslist(bank, oc, which, last=False):
        pe(bank, [(X(bank, oc, oc + 64)[0], T.L[:, 16 * a + 1 - h:16 * a + 17 - h, :], T.id1[:, :, h::2]) for a in which for h in range(2)],
           [lists(a) for a in which] + [ID], last)

    dma("S", T.hl[:, 0:V0], T.h0[:, I:I + V0], [], [X("hl", 0, V0)])
    dma("A", T.si[:, 0:42], T.sl[:, :], [], [X("si", 0, 42)])
    dma("S", T.KI[:, 0:64], T.kl[:, :], [], [X("KI", 0, 64)])
    dma("A", T.KI[:, 64:128], T.kr[:, :], [], [X("KI", 64, 128)])
    dma("S", T.vi[:, 0:V0], T.vel[:, :], [], [X("vi", 0, V0)])
    dma("S", T.hi[:, :], T.h0[:, 0:I], [], [X("hi", 0, 1024)])

    vset(X("ones", 0, 128), 1.0)
    giota(X("nrow", 0, 512), [[1, 512]], 1024, 0)
    act(X("PA", D, D + 128), X("ones", 0, 128), AF.Silu, scale=0.0)
    vset(X("PW", D, OWN), 0.0)
    act(X("nrow", 512, 1024), X("nrow", 0, 512), bias=512.0)
    act(X("PA", D + 128, D + 640), X("nrow", 0, 512), scale=0.0)
    act(X("PA", D + 640, OWN), X("nrow", 0, 384), scale=0.0)
    gsel(ID, X("ones", 0, 128), [[-1, 128]], OP.is_equal, 0, 1)
    giota(X("nf", 0, 64), [[0, 8], [1, 8]], 1024, 8)
    giota(X("BS", 0, 16), [[-2, 2], [0, 8]], 1, 0)
    giota(X("H0", 0, D), [[0, D]], 0, 0)
    gsel(X("BS", 0, 16), X("BS", 0, 16), [[0, 2], [-16, 8]], OP.is_ge, 0, 1)
    gsel(X("O32", 0, 8), X("ones", 0, 8), [[-16, 8]], OP.is_equal, 0, 1)
    gsel(X("BS", 0, 16), X("BS", 0, 16), [[0, 2], [16, 8]], OP.is_ge, 15, -1)
    vset(X("KW", 0, 272), 0.0)
    emit("V", [lambda: g.vector.memset(T.L[:, 0:193:2, :], 0.0)], [], [(None, "L", 0, 1544)])
    vcopy(X("su", 0, 42), X("si", 0, 42))
    for call in sends(T, topo, rank, True):
        for d in sorted(call):
            if d - 1 not in call:
                e = min(x for x in range(d, 9) if x not in call)
                vcopy(X("s0", GH * (d - 1), GH * (e - 1)), ind(X("hl", 0, V0), X("su", 6 * (d - 1), 6 * (e - 1))))
    vts(X("KU", 0, 128), X("KI", 0, 128), float(D), OP.add)

    nsent = [0]
    for r in range(RO):
        narr = sum(len(call[d]) for d in range(1, 8) for call in sends(T, topo, (rank - d) % 8, r == 0) if d in call)
        cnt["arr%d" % r] = narr
        acc.setdefault("H%d" % r, []).append((True, GHO, WIN, ("arr%d" % r, narr, "R", {})))

    def exchange(r):
        for call in sends(T, topo, rank, r == 0):
            sync("G", hazards("G", [X("s%d" % r, GH * (d - 1), GH * d) for d in call], []))
            tr = []
            for d, engines in call.items():
                rid, pid, _ = topo.addr(T.cores[(rank + d) % 8])
                tr.append(RemoteDMATransfer(src=T["s%d" % r][:, GH * (d - 1):GH * d],
                                            dst=T["H%d" % r][:, GHO + GH * (d - 1):GHO + GH * d], dst_ids=[DstId(rid=rid, pnc=pid)],
                                            dma_engine_mask=sum(1 << e for e in engines), remote_sem=T.sem["arr%d" % r]))
                nsent[0] += len(engines)
            g.remote_dma_fused(tr, local_sem=T.sem.sent)
    exchange(0)

    emit("A", [lambda: g.scalar.activation(T.PA[:, 0:WIN].indirect(T.KU[:, 64:128]), T.nrow[:, :], AF.Silu)],
         [X("nrow", 0, 1024), X("KU", 64, 128)], [X("PA", 0, WIN)])
    vcopy(X("H0", OWN, GHO), X("hl", 0, V0))
    vcopy(X("vo", 0, V0), X("vi", 0, V0))
    vcopy(ind(X("PW", 0, WIN), X("KU", 0, 64)), X("nrow", 0, 1024))
    vset(X("H1", I, OWN), 0.0)
    vts(X("su", 0, 42), X("si", 0, 42), float(D), OP.add)
    for s in range(2):
        vcopy(X("KW", 136 * s + 1, 136 * s + 129, 2), X("KI", 64 * s, 64 * s + 64))
    vcopy(X("H0", D, OWN), X("hi", 0, I))
    for j in range(2):
        vts(X("nid", 64 * j, 64 * j + 64), X("nf", 0, 64), -1024.0, OP.add)
    vts(X("KC", 0, 128), X("KU", 0, 128), float(OWN), OP.min)
    for nm in ("hcl", "hcr"):
        vset(X(nm, 0, D), 0.0)
        vset(X(nm, OWN, OWN + 1), 255.0)
    giota(X("CQ", 0, 256), [[0, 64], [1, 4]], 0, 0)
    gsel(X("msk", 0, 256), X("CQ", 0, 256), [[0, 64], [-1, 4]], OP.is_ge, 0, 0, 1.0)
    giota((T.XG[:, :, 8:16, :], "XG", 8, 16), [[0, 512]], 0, 0)
    diagonal(("idq", -0.25))
    for nm in ("GW", "CW"):
        giota(X(nm, OWN, OWN + 1), [[0, 1]], 0, 0)
    for nm in ("GW", "CW", "H1", "H2"):
        giota(X(nm, 0, D), [[0, D]], 0, 0)
    giota(X("H2", I, OWN), [[0, D]], 0, 0)

    def moved(r):
        plus("b1", [(0, V0, "id1", X("H%d" % r, OWN, GHO)), (0, V0, "id1", X("vo", 0, V0))], True)

    def leaves(r):
        act(X("y1", 0, V0), X("b1", 0, V0), AF.Relu, scale=-1.0, bias=255.0)
        act(X("OH", I, I + V0) if r == RO - 1 else X("H%d" % (r + 1), OWN, GHO), X("y1", 0, V0), AF.Relu, scale=-1.0, bias=255.0)

    def ghosts(r):
        act(X("s%d" % r, 0, 672), ind(X("H%d" % r, I, GHO), X("su", 0, 42)))

    moved(0)
    leaves(0)
    gsel(X("WP", 0, 32), X("ones", 0, 32), [[-2, 4], [-16, 8]], OP.is_ge, 0, 1)
    gsel(X("OC", 0, 8), X("ones", 0, 8), [[-16, 8]], OP.is_equal, -10, 1)
    gsel(X("WP", 0, 32), X("WP", 0, 32), [[2, 4], [16, 8]], OP.is_ge, 1, -1)
    ghosts(1)

    NID = X("nid", 0, 64)
    ONE = X("ones", 0, 64)

    def rounded(p, bank, oc):
        act(part("XG", p), X(bank, oc, oc + 64))

    def rest(p, bank, oc):
        vtt(part("XG", p + 1), X(bank, oc, oc + 64), part("XG", p), OP.subtract)

    pe("b5", [(T.b5[:, 64 * s:64 * s + 64], T.KW[:, 136 * s + 1 - h:136 * s + 129 - h], T.id1[:, h::2, :])
              for s in range(2) for h in range(2)], [X("KW", 0, 272), ID], True)
    rounded(2, "b5", 0)
    rounded(4, "b5", 64)
    wrap("b6", 64, "PA", D, X("O32", 0, 8))
    wrap("b6", 64, "PW", D, X("O32", 0, 8), True)

    def gcopy(out, in_):
        gsel(out, in_, [[0, in_[3] - in_[2]]], OP.is_ge, 0, 0)

    BSP, BSN = X("BS", 0, 8), X("BS", 8, 16)
    GA = X("gq", 3, 256, 4)
    ROT, CHOICE, SIDE = part("XG", 8), X("cd", 0, 64), part("XG", 10)
    NA = 512
    for r in range(RO):
        last = r == RO - 1
        win = X("H%d" % r, 0, WIN)
        wl, wr = X("hcl", 0, OWN + 1), X("hcr", 0, OWN + 1)

        act(X("hcl", D, OWN), ind(win, X("KU", 0, 64)))
        vcopy(X("hcr", D, OWN), ind(win, X("KU", 64, 128)))
        if r:
            vts(X("E2", 0, 192), X("b3", 0, 192), 0.0, OP.is_equal)
            rest(2, "b5", 0)
            vtt(lists(W0, 3), X("b7", 256, 448), X("E2", 0, 192), OP.mult)
        else:
            vts(X("idn", 0, 128), ID, -1.0, OP.mult)
            vcopy(part("XG", 6), X("b6", 64, 128))
        (gcopy if r else vcopy)(X("hr2", NA, 1024), X("hcr", D + NA, OWN))
        if not r:
            giota(X("sPP", 0, 144), [[0, 144]], 0, 0)
            gsel(X("WG", 16, 48), X("ones", 0, 32), [[0, 4], [-16, 8]], OP.is_ge, -2, 1)
            diagonal(("idk", 1024.0), ("ide", 2.0 ** -13), ("idf", -2.0 ** -13))
            gcopy(X("WG", 0, 8), X("WP", 0, 8))
            gcopy(X("WG", 8, 16), X("WP", 16, 24))
            gcopy(X("WG", 48, 56), X("WP", 24, 32))
            gsel(X("WG", 16, 48), X("WG", 16, 48), [[0, 4], [16, 8]], OP.is_ge, 5, -1)
            gcopy(X("WR", 8, 24), X("WP", 8, 24))
            gsel(X("sPP", 16, 144, 16), X("WP", 24, 32), [[0, 8]], OP.is_ge, 0, 0)
            exchange(1)
            diagonal(("idh", 0.5), ("idhn", -0.5))
            giota(X("WC", 0, 32), [[0, 4], [-32, 8]], -17, 2)
            gsel(X("WC", 0, 32), X("WC", 0, 32), [[0, 4], [-16, 8]], OP.is_ge, -8, 1)
            giota(X("CE", 0, 256), [[1, 4], [0, 64]], -4, 0)
            gsel(X("WC", 0, 32), X("WC", 0, 32), [[0, 4], [16, 8]], OP.is_ge, 9, -1)
        if not last:
            moved(r + 1)
        act(X("zz", 0, 512), ind(wl, X("KC", 64, 96)))
        act(X("zz", 512, 1024), ind(wl, X("KC", 96, 128)))
        act(X("zz", 1024, 1024 + NA), ind(wr, X("KC", 0, NA // 16)))
        vtt(X("mm", 1024, 2048), ind(wl, X("KC", 0, 64)), X("hcr", D, OWN), OP.max)
        vtt(X("mm", 2048, 3072), ind(wr, X("KC", 64, 128)), X("hcl", D, OWN), OP.max)
        vtt(X("mm", NA, 1024), ind(wr, X("KC", NA // 16, 64)), X("hr2", NA, 1024), OP.max)
        if r:
            plus("b4", [(0, 256, "idq", X("CQ", 0, 256))])
        gain("hcr", D, BSP, 2)
        gain("hcr", D, BSP, 3)
        gain("hcl", D, BSP, 0)
        plus("b0", [(0, 512, "idn", X("hcl", D, D + 512)), (0, 512, "id1", X("zz", 0, 512))], True)
        if r:
            plus("b6", [(64, 64, "id1", lists(a)) for a in (PAR, W0, W1, XX)], True)
        gain("hcl", D, BSP, 1)
        plus("b3", [(0, 512, "idn", X("hcl", D + 512, OWN)), (0, 512, "id1", X("zz", 512, 1024))], True)
        gain("hcl", D, BSN, 3)
        gain("hcr", D, BSN, 0, False, NA // 8)
        if not r:
            plus("b4", [(0, 256, "idq", X("CQ", 0, 256))])
        plus("b2", [(0, NA, "idn", X("hcr", D, D + NA)), (0, NA, "id1", X("zz", 1024, 1024 + NA))], True)
        act(X("mm", 3072, 3584), X("b0", 0, 512), AF.Relu)
        if r == 1:
            rounded(6, "b6", 64)
        gain("mm", 1024, BSN, 1)
        act(X("mm", 3584, 4096), X("b3", 0, 512), AF.Relu)
        act(X("mm", 0, NA), X("b2", 0, NA), AF.Relu)
        gain("mm", 2048, BSN, 2)
        gain("mm", 3072, BSN, 3)
        gain("mm", 0, BSN, 0, True)
        if not last:
            leaves(r + 1)
        if not r:
            act(X("WC", 32, 40), X("OC", 0, 8), scale=-0.5)
            act(X("WR", 0, 8), X("WP", 0, 8), scale=-2.0 ** -13)
        if r == 1:
            dma("S", T.yh[:, I:I + V0], T.OH[:, I:I + V0], [X("OH", I, I + V0)], [])
        vcopy(lists(PAR), X("b6", 64, 128))
        if not r:
            rest(2, "b5", 0)
        rest(4, "b5", 64)
        vcopy(lists(KL, 2), X("b5", 0, 128))
        if r == 1:
            rest(6, "b6", 64)
        elif not r:
            vtt(part("XG", 7), lists(PAR), part("XG", 6), OP.subtract)
        emit("V", [lambda: g.vector.tensor_tensor_scan(T.gq[:, :], T.msk[:, :], T.b4[:, 0:256], 0.0, OP.mult, OP.max)],
             [X("msk", 0, 256), X("b4", 0, 256)], [X("gq", 0, 256)])
        vtt(X("TB", 128, 192), X("b6", 64, 128), X("nf", 0, 64), OP.is_gt)
        aslist("b6", 0, (PAR,), True)
        vcopy(part("XG", 0), GA)
        vts(X("gi", 0, 64), GA, 0.375, OP.add)
        vtt(part("XG", 1), GA, part("XG", 0), OP.subtract)
        spread("XG", 0)
        spread("XG", 1)
        vts(X("PB", 0, 64), X("b6", 0, 64), D - 1024.0, OP.add, 0.0, OP.max)
        vtt(X("TB", 0, 128), X("b5", 0, 128), X("nid", 0, 128), OP.is_gt)
        vtt(CHOICE, X("gi", 0, 64), GA, OP.subtract)
        act(X("GW", D, D + 512), X("b0", 0, 512))
        vcopy(X("GW", D + 512, OWN), X("b1", 0, 512))
        gwin = X("GW", 0, OWN + 1)
        plus("b7", [(0, 64, "id1", X("TB", 128, 192)), (128, 128, "idn", lists(KL, 2)), (64, 64, "idn", NID),
                    (128, 128, "idn", X("nid", 0, 128))])
        if not last:
            plus("b7", [(256, 128, "idk", X("ones", 0, 128)), (256, 128, "idn", X("nid", 0, 128))]
                 + [(oc, 64, "idn", lists(PAR)) for oc in (256, 320, 384)])
        plus("b5", [(0, 64, "id1", X("TB", 0, 64)), (64, 64, "idn", lists(KR)), (128, 64, "idn", lists(KR))])
        plus("b6", [(0, 64, "ide", part("XG", 0)), (0, 64, "ide", part("XG", 1)), (0, 64, "ide", CHOICE),
                    (0, 64, "idf", X("TB", 64, 128)), (64, 64, "idn", lists(KL)), (128, 64, "idn", lists(KL))])

        def both(buf, w, lst, o, cut):
            act(X(buf, 0, cut), ind(w, X(lst, o, o + cut // 16)))
            vcopy(X(buf, cut, 1024), ind(w, X(lst, o + cut // 16, o + 64)))

        both("gp", gwin, "PB", 0, 512)
        both("gl", gwin, "KC", 0, 512)
        both("gr", gwin, "KC", 64, 512)
        wrap("b7", 0, "gp", 0, X("WG", 0, 32 if last else 56), True)
        if not last:
            pe("b4", [(T.b4[:, 256:320], T.sPP[:, 16 - k:144 - k], T.gp[:, k:1024:16]) for k in range(16)],
               [X("sPP", 0, 144), X("gp", 0, 1024)], True)
        wrap("b5", 0, "gl", 0, X("WP", 0, 24), True)
        wrap("b6", 0, "gr", 0, X("WR", 0, 24), True)
        act(part("XG", 9), CHOICE)
        if not r:
            ghosts(2)
            exchange(2)
        vts(X("ee", 0, 64), X("b7", 0, 64), 1.0, OP.max)
        vts(SIDE, X("b7", 64, 128), 0.0, OP.is_equal)
        vtt(X("ee", 64, 128), X("b5", 0, 64), X("ee", 0, 64), OP.max)
        if not last:
            vts(X("PPu", 0, 64), X("b4", 256, 320), D - 1024.0, OP.add, 0.0, OP.max)
        vtt(X("ee", 128, 192), X("ee", 64, 128), X("gi", 0, 64), OP.is_gt)
        vtt(ROT, X("b6", 0, 64), X("ee", 128, 192), OP.is_ge)
        spread("XG", 0)
        spread("XG", 1)
        vtt(X("cod", 0, 64), CHOICE, ROT, OP.subtract)
        for j in range(4):
            vts(X("MK", 64 * j, 64 * j + 64), X("cod", 0, 64), 0.25 * j - 1.0, OP.is_equal)
        act(X("CW", D, D + 512), X("b0", 0, 512))
        vcopy(X("CW", D + 512, OWN), X("b1", 0, 512))
        cwin = X("CW", 0, OWN + 1)
        plus("b2", [(0, 128, "idq", X("CE", 0, 128)), (0, 64, "idhn", SIDE), (64, 64, "idhn", SIDE)])
        both("cp", cwin, "PB", 0, 512)
        aslist("b4", 0, (KR,))
        if not last:
            plus("b3", [(0, 128, "idq", X("CE", 128, 256)), (128, 64, "id1", ONE), (0, 64, "idh", SIDE), (64, 64, "idh", SIDE),
                        (128, 64, "idq", SIDE)])
        wrap("b2", 0, "cp", 0, X("WC", 0, 16), True)
        vtt(lists(P0, 2), X("b5", 64, 192), X("MK", 0, 128), OP.mult)
        vtt(lists(P2, 2), X("b6", 64, 192), X("MK", 128, 256), OP.mult)
        aslist("b4", 0, (P0, P1))
        aslist("b1", 0, (KL, P2, P3))
        if not last:
            act(X("cg", 0, CG), ind(cwin, X("PPu", 0, CG // 16)))
        vts(X("E1", 64, 128), X("b2", 64, 128), 0.0, OP.is_equal)
        vts(X("E1", 0, 64), X("b2", 0, 64), 0.0, OP.is_equal)
        vtt(lists(TR), X("b7", 192, 256), X("E1", 64, 128), OP.mult)
        vtt(lists(TL), X("b7", 128, 192), X("E1", 0, 64), OP.mult)
        aslist("b4", 0, (TR,), True)
        aslist("b1", 0, (TL,), True)
        plus("b5", [(0, 128, "id1", lists(KL, 2)), (0, 64, "id1", lists(P2)), (0, 64, "id1", lists(P3)),
                    (64, 64, "id1", lists(P0)), (64, 64, "id1", lists(P1)), (0, 128, "id1", lists(TL, 2))], True)
        vts(X("KU", 64, 128), X("b4", 0, 64), float(D), OP.add)
        vts(X("KU", 0, 64), X("b1", 0, 64), float(D), OP.add)
        cuts = (0, 128, 448, 768, 1024) if last else CUTS
        for j, (a, b) in enumerate(zip(cuts, cuts[1:])):
            (act if j else vcopy)(X("rr", a, b), ind(win, X("KU", 64 + a // 16, 64 + b // 16)))
        if not last:
            vts(X("KC", 0, 128), X("KU", 0, 128), float(OWN), OP.min)
        else:
            vcopy(lists(KL, 2), X("b5", 0, 128))
            for h in range(2):
                pe("b0", [(T.b0[64 * h:64 * h + 64, b:512:8], T.L[:, 1:129:2, b], T.id1[:, 8 * h:8 * h + 8, :]) for b in range(8)],
                   [lists(KL, 8), ID], True)
            act(X("OK", 0, 512), X("b0", 0, 512))
            for h in range(2):
                for s in range(2):
                    dma("A", T.yk[:, 1024 * s + 512 * h:1024 * s + 512 * h + 512], T.OK[64 * h + 8 * s:64 * h + 8 * s + 8, 0:512],
                        [X("OK", 0, 512)], [])
        if not last:
            wrap("b3", 0, "cp", 0, X("WC", 16, 40))
            act(X("cg", CG, 1024), ind(cwin, X("PPu", CG // 16, 64)))
            wrap("b3", 128, "cg", 0, X("WC", 0, 8), True)
            rounded(2, "b5", 0)
            rounded(4, "b5", 64)
        for a, b in zip(cuts, cuts[1:]):
            vtt(X("OH", a, b) if last else X("H%d" % (r + 1), D + a, D + b), ind(win, X("KU", a // 16, b // 16)), X("rr", a, b), OP.max)
            if last:
                dma("S", T.yh[:, a:b], T.OH[:, a:b], [X("OH", a, b)], [])

    cnt["sent"] = nsent[0]
    for s, c in cnt.items():
        g.wait_ge(T.sem[s], c)
